import numpy as np
import ml_dtypes


def mxq(x, axis, fmt="e4m3"):
    dtype, down = {"e4m3": (ml_dtypes.float8_e4m3fn, 7), "e5m2": (ml_dtypes.float8_e5m2, 14)}[fmt]
    v = np.moveaxis(np.asarray(x, np.float32).astype(ml_dtypes.bfloat16).astype(np.float64), axis, -1)
    blocks = v.reshape(v.shape[:-1] + (-1, 32))
    amax = np.abs(blocks).max(-1, keepdims=True)
    byte = np.maximum(np.where(amax > 0, np.frexp(amax)[1] - 1 + 127, 0) - down, 1)
    scale = np.exp2(byte - 127.0)
    codes = (blocks / scale).astype(np.float32).astype(dtype).astype(np.float64)
    return np.moveaxis((codes * scale).reshape(v.shape), -1, axis)


WIDE = False


def mx_kscale(k):
    if not WIDE:
        return np.ones(k)
    levels = np.array([10, -10, 5, -5, 0])
    if k % 512:
        return np.exp2(np.random.permutation(np.resize(levels, k // 32))).repeat(32)
    a = np.empty((k // 512, 16))
    for p in range(k // 512):
        a[p, :8] = np.random.permutation(np.resize(levels, 8))
        for g in range(8):
            far = levels[np.abs(levels - a[p, g]) >= 10]
            a[p, g + 8] = far[np.random.randint(len(far))]
    return np.exp2(a.ravel()).repeat(32)


def f64(x):
    return np.asarray(x).astype(np.float64)


def striped(idx):
    return np.tile(idx.reshape(-1, 16).T, (8, 1)).astype(np.uint16)


def unstriped(offs):
    return offs[:16].T.reshape(-1).astype(np.int64)


def pack_weight(w):
    k, n = w.shape
    w = f64(np.asarray(w, np.float32).astype(ml_dtypes.bfloat16)).reshape(k // 32, 32, n)
    amax = np.abs(w).max(1)
    byte = np.clip(np.where(amax > 0, np.frexp(amax)[1] - 1 + 127 - 7, 1), 1, 254)
    scaled = (w * np.exp2(127.0 - byte)[:, None, :]).reshape(k, n).astype(np.float32)
    words = np.ascontiguousarray(scaled.reshape(k // 512, 128, 4, n).transpose(0, 1, 3, 2)).astype(ml_dtypes.float8_e4m3fn).view(np.uint8)
    return words, np.ascontiguousarray(byte.astype(np.uint8).reshape(k // 512, 16, n))


def unpack_weight(words, scales):
    g, p, n, _ = words.shape
    vals = np.ascontiguousarray(words).view(ml_dtypes.float8_e4m3fn).astype(np.float64) * np.repeat(np.exp2(scales.astype(np.float64) - 127.0), 8, axis=1)[..., None]
    return vals.transpose(0, 1, 3, 2).reshape(g * 512, n)


K, T, S, N = 1024, 2048, 512, 256


def setup_inputs():
    n = np.random.standard_normal
    s = mx_kscale(K)[:, None]
    packed_w1 = pack_weight(n((K, N)) / np.sqrt(K) / s)
    packed_w2 = pack_weight(n((K, N)) / np.sqrt(K) / s)
    packed_w3 = pack_weight(n((K, N)) / np.sqrt(K) / s)
    return {
        "xT": (n((K, T)) * s).astype(np.float32),
        "w1_words": packed_w1[0],
        "w1_scales": packed_w1[1],
        "w2_words": packed_w2[0],
        "w2_scales": packed_w2[1],
        "w3_words": packed_w3[0],
        "w3_scales": packed_w3[1],
        "offs": striped(np.random.permutation(T)[:S]),
    }


def reference(xT, w1_words, w1_scales, w2_words, w2_scales, w3_words, w3_scales, offs):
    xq = mxq(f64(xT)[:, unstriped(offs)], 0, "e4m3")
    return np.maximum(np.maximum(unpack_weight(w1_words, w1_scales).T @ xq, unpack_weight(w2_words, w2_scales).T @ xq), unpack_weight(w3_words, w3_scales).T @ xq)

@@ -1,0 +1,111 @@
+from contextlib import ExitStack
+
+import concourse.mybir as mybir
+
+K, T, S, N = 1024, 2048, 512, 256
+FLOPS = 3 * 2 * K * S * N
+
+F32 = mybir.dt.float32
+BF16 = mybir.dt.bfloat16
+I32 = mybir.dt.int32
+U32 = mybir.dt.uint32
+U16 = mybir.dt.uint16
+U8 = mybir.dt.uint8
+FP8X4 = mybir.dt.float8_e4m3fn_x4
+MAX = mybir.AluOpType.max
+
+P = 128
+PACK = 4
+PASSES = K // (P * PACK)
+HALVES = 2
+HALF = S // HALVES
+M_TILES = N // P
+QUADS = 4
+
+
+def tile_picked_maxout_max_e_kernel(
+    tc, xT, w1_words, w1_scales, w2_words, w2_scales, w3_words, w3_scales, offs, out
+):
+    nc = tc.nc
+    words_in = (w1_words, w2_words, w3_words)
+    scales_in = (w1_scales, w2_scales, w3_scales)
+    x_rows = xT.rearrange("(z p t) n -> z t p n", z=PASSES, t=PACK)
+
+    with ExitStack() as ctx:
+        keep = ctx.enter_context(tc.tile_pool(name="keep", bufs=1))
+        psum = ctx.enter_context(tc.psum_pool(name="psum", bufs=8))
+
+        offsets = keep.tile([P, S // 16], U16, name="offsets")
+        planes = {}
+        for z in range(PASSES):
+            for t in range(PACK):
+                planes[z, t] = keep.tile([P, T], F32, name=f"plane{z}{t}", align_bytes=64)
+                nc.sync.dma_start(out=planes[z, t][:], in_=x_rows[z, t])
+                if (z, t) == (0, 0):
+                    nc.sync.dma_start(offsets[:], offs)
+
+        w_codes, w_scales = [], []
+        for w in range(3):
+            codes = keep.tile([P, PASSES, N], U32, name=f"w_codes{w}", align_bytes=64)
+            nc.sync.dma_start(
+                out=codes[:].bitcast(I32),
+                in_=words_in[w].rearrange("z p n t -> p z (n t)").bitcast(I32),
+            )
+            w_codes.append(codes)
+            scales = keep.tile([P, PASSES, N], U8, name=f"w_scales{w}", align_bytes=64)
+            nc.vector.memset(scales[:].bitcast(I32), 0)
+            for q in range(QUADS):
+                nc.gpsimd.dma_start(
+                    out=scales[32 * q : 32 * q + 4, :, :].bitcast(I32),
+                    in_=scales_in[w][:, 4 * q : 4 * q + 4, :].rearrange("z r n -> r z n").bitcast(I32),
+                )
+            w_scales.append(scales)
+
+        x_codes, x_scales = {}, {}
+        cols = HALF // 16
+        for z in range(PASSES):
+            picked = [keep.tile([P, HALF, PACK], BF16, name=f"picked{z}{h}", align_bytes=64) for h in range(HALVES)]
+            for t in range(PACK):
+                for h in range(HALVES):
+                    nc.vector.tensor_copy(
+                        out=picked[h][:, :, t],
+                        in_=planes[z, t][:].indirect(offsets[:, h * cols : (h + 1) * cols]),
+                    )
+            for h in range(HALVES):
+                x_codes[z, h] = keep.tile([P, HALF], U32, name=f"x_codes{z}{h}", align_bytes=64)
+                x_scales[z, h] = keep.tile([P, HALF], U8, name=f"x_scales{z}{h}", align_bytes=64)
+                nc.vector.quantize_mx(
+                    out=x_codes[z, h][:].bitcast(FP8X4),
+                    scales=x_scales[z, h][:],
+                    in_=picked[h][:].rearrange("p n t -> p (n t)"),
+                )
+
+        for h in range(HALVES):
+            acc = {}
+            for w in range(3):
+                for m in range(M_TILES):
+                    acc[w, m] = psum.tile([P, HALF], F32, name="acc")
+            for z in range(PASSES):
+                for w in range(3):
+                    for m in range(M_TILES):
+                        rows = slice(m * P, (m + 1) * P)
+                        nc.tensor.matmul_mx(
+                            out=acc[w, m][:],
+                            lhsT=w_codes[w][:, z, rows].bitcast(FP8X4),
+                            lhsT_scale=w_scales[w][:, z, rows],
+                            rhs=x_codes[z, h][:].bitcast(FP8X4),
+                            rhs_scale=x_scales[z, h][:],
+                            start=(z == 0),
+                            stop=(z == PASSES - 1),
+                        )
+            first, two, three = {}, {}, {}
+            for m in range(M_TILES):
+                first[m] = keep.tile([P, HALF], F32, name=f"first{h}{m}")
+                nc.scalar.copy(out=first[m][:], in_=acc[0, m][:])
+            for m in range(M_TILES):
+                two[m] = keep.tile([P, HALF], F32, name=f"two{h}{m}")
+                nc.vector.tensor_tensor(two[m][:], acc[1, m][:], first[m][:], MAX)
+            for m in range(M_TILES):
+                three[m] = keep.tile([P, HALF], F32, name=f"three{h}{m}")
+                nc.vector.tensor_tensor(three[m][:], acc[2, m][:], two[m][:], MAX)
+                nc.sync.dma_start(out=out[m * P : (m + 1) * P, h * HALF : (h + 1) * HALF], in_=three[m][:])

@@ -36,6 +36,7 @@ def tile_picked_maxout_max_e_kernel(
         psum = ctx.enter_context(tc.psum_pool(name="psum", bufs=8))
 
         offsets = keep.tile([P, S // 16], U16, name="offsets")
+        staged = keep.tile([16, 3, PASSES, N], U8, name="staged", align_bytes=64)
         planes = {}
         for z in range(PASSES):
             for t in range(PACK):
@@ -43,8 +44,13 @@ def tile_picked_maxout_max_e_kernel(
                 nc.sync.dma_start(out=planes[z, t][:], in_=x_rows[z, t])
                 if (z, t) == (0, 0):
                     nc.sync.dma_start(offsets[:], offs)
+                    for w in range(3):
+                        nc.sync.dma_start(
+                            out=staged[:, w, :, :].bitcast(I32),
+                            in_=scales_in[w].rearrange("z q n -> q z n").bitcast(I32),
+                        )
 
-        w_codes, w_scales = [], []
+        w_codes = []
         for w in range(3):
             codes = keep.tile([P, PASSES, N], U32, name=f"w_codes{w}", align_bytes=64)
             nc.sync.dma_start(
@@ -52,33 +58,55 @@ def tile_picked_maxout_max_e_kernel(
                 in_=words_in[w].rearrange("z p n t -> p z (n t)").bitcast(I32),
             )
             w_codes.append(codes)
-            scales = keep.tile([P, PASSES, N], U8, name=f"w_scales{w}", align_bytes=64)
-            nc.vector.memset(scales[:].bitcast(I32), 0)
-            for q in range(QUADS):
-                nc.gpsimd.dma_start(
-                    out=scales[32 * q : 32 * q + 4, :, :].bitcast(I32),
-                    in_=scales_in[w][:, 4 * q : 4 * q + 4, :].rearrange("z r n -> r z n").bitcast(I32),
-                )
-            w_scales.append(scales)
+
+        w_scales = keep.tile([P, 3 * PASSES * N], U8, name="w_scales", align_bytes=64)
+        nc.gpsimd.memset(w_scales[:].bitcast(I32), 0)
+        for q in range(QUADS):
+            nc.gpsimd.dma_start(
+                out=w_scales[32 * q : 32 * q + 4, :].bitcast(I32),
+                in_=staged[4 * q : 4 * q + 4, :, :, :].rearrange("r w z n -> r (w z n)").bitcast(I32),
+            )
 
         x_codes, x_scales = {}, {}
         cols = HALF // 16
-        for z in range(PASSES):
-            picked = [keep.tile([P, HALF, PACK], BF16, name=f"picked{z}{h}", align_bytes=64) for h in range(HALVES)]
-            for t in range(PACK):
-                for h in range(HALVES):
-                    nc.vector.tensor_copy(
-                        out=picked[h][:, :, t],
-                        in_=planes[z, t][:].indirect(offsets[:, h * cols : (h + 1) * cols]),
-                    )
+
+        rows0 = keep.tile([P, PACK, S], BF16, name="rows0", align_bytes=64)
+        for t in range(PACK):
+            nc.vector.tensor_copy(out=rows0[:, t, :], in_=planes[0, t][:].indirect(offsets[:]))
+        picked0 = keep.tile([P, S, PACK], BF16, name="picked0", align_bytes=64)
+        nc.scalar.copy(out=picked0[:], in_=rows0[:].rearrange("p t n -> p n t"))
+        codes0 = keep.tile([P, S], U32, name="codes0", align_bytes=64)
+        scales0 = keep.tile([P, S], U8, name="scales0", align_bytes=64)
+        nc.vector.quantize_mx(
+            out=codes0[:].bitcast(FP8X4), scales=scales0[:], in_=picked0[:].rearrange("p n t -> p (n t)")
+        )
+        for h in range(HALVES):
+            x_codes[0, h] = codes0[:, h * HALF : (h + 1) * HALF]
+            x_scales[0, h] = scales0[:, h * HALF : (h + 1) * HALF]
+
+        rows1 = keep.tile([P, 2, S], BF16, name="rows1", align_bytes=64)
+        for t in range(2):
+            nc.vector.tensor_copy(out=rows1[:, t, :], in_=planes[1, t][:].indirect(offsets[:]))
+        picked1 = [keep.tile([P, HALF, PACK], BF16, name=f"picked1{h}", align_bytes=64) for h in range(HALVES)]
+        for h in range(HALVES):
+            nc.scalar.copy(
+                out=picked1[h][:, :, 0:2],
+                in_=rows1[:, :, h * HALF : (h + 1) * HALF].rearrange("p t n -> p n t"),
+            )
+        for t in range(2, PACK):
             for h in range(HALVES):
-                x_codes[z, h] = keep.tile([P, HALF], U32, name=f"x_codes{z}{h}", align_bytes=64)
-                x_scales[z, h] = keep.tile([P, HALF], U8, name=f"x_scales{z}{h}", align_bytes=64)
-                nc.vector.quantize_mx(
-                    out=x_codes[z, h][:].bitcast(FP8X4),
-                    scales=x_scales[z, h][:],
-                    in_=picked[h][:].rearrange("p n t -> p (n t)"),
+                nc.vector.tensor_copy(
+                    out=picked1[h][:, :, t],
+                    in_=planes[1, t][:].indirect(offsets[:, h * cols : (h + 1) * cols]),
                 )
+        for h in range(HALVES):
+            codes1 = keep.tile([P, HALF], U32, name=f"codes1{h}", align_bytes=64)
+            scales1 = keep.tile([P, HALF], U8, name=f"scales1{h}", align_bytes=64)
+            nc.vector.quantize_mx(
+                out=codes1[:].bitcast(FP8X4), scales=scales1[:], in_=picked1[h][:].rearrange("p n t -> p (n t)")
+            )
+            x_codes[1, h] = codes1[:]
+            x_scales[1, h] = scales1[:]
 
         for h in range(HALVES):
             acc = {}
@@ -89,12 +117,13 @@ def tile_picked_maxout_max_e_kernel(
                 for w in range(3):
                     for m in range(M_TILES):
                         rows = slice(m * P, (m + 1) * P)
+                        first_byte = (w * PASSES + z) * N + m * P
                         nc.tensor.matmul_mx(
                             out=acc[w, m][:],
                             lhsT=w_codes[w][:, z, rows].bitcast(FP8X4),
-                            lhsT_scale=w_scales[w][:, z, rows],
-                            rhs=x_codes[z, h][:].bitcast(FP8X4),
-                            rhs_scale=x_scales[z, h][:],
+                            lhsT_scale=w_scales[:, first_byte : first_byte + P],
+                            rhs=x_codes[z, h].bitcast(FP8X4),
+                            rhs_scale=x_scales[z, h],
                             start=(z == 0),
                             stop=(z == PASSES - 1),
                         )

@@ -21,6 +21,8 @@ HALVES = 2
 HALF = S // HALVES
 M_TILES = N // P
 QUADS = 4
+WARM = 3
+ORDER = [(0, 0), (0, 1), (0, 2), (1, 0), (1, 1), (0, 3), (1, 2), (1, 3)]
 
 
 def tile_picked_maxout_max_e_kernel(
@@ -36,19 +38,22 @@ def tile_picked_maxout_max_e_kernel(
         psum = ctx.enter_context(tc.psum_pool(name="psum", bufs=8))
 
         offsets = keep.tile([P, S // 16], U16, name="offsets")
-        staged = keep.tile([16, 3, PASSES, N], U8, name="staged", align_bytes=64)
+        w_scales = keep.tile([P, PASSES, N], U8, name="w_scales", align_bytes=64)
+        nc.vector.memset(w_scales[:].bitcast(I32), 0)
         planes = {}
-        for z in range(PASSES):
-            for t in range(PACK):
-                planes[z, t] = keep.tile([P, T], F32, name=f"plane{z}{t}", align_bytes=64)
-                nc.sync.dma_start(out=planes[z, t][:], in_=x_rows[z, t])
-                if (z, t) == (0, 0):
-                    nc.sync.dma_start(offsets[:], offs)
-                    for w in range(3):
-                        nc.sync.dma_start(
-                            out=staged[:, w, :, :].bitcast(I32),
-                            in_=scales_in[w].rearrange("z q n -> q z n").bitcast(I32),
-                        )
+        for i, (z, t) in enumerate(ORDER):
+            planes[z, t] = keep.tile([P, T], F32, name=f"plane{z}{t}", align_bytes=64)
+            nc.sync.dma_start(out=planes[z, t][:], in_=x_rows[z, t])
+            if (z, t) == ORDER[0]:
+                nc.sync.dma_start(offsets[:], offs)
+            if 2 <= i < 5:
+                w = i - 2
+                for q in range(QUADS):
+                    row = 32 * q + 4 * w
+                    nc.sync.dma_start(
+                        out=w_scales[row : row + 4, :, :].bitcast(I32),
+                        in_=scales_in[w][:, 4 * q : 4 * q + 4, :].rearrange("z r n -> r z n").bitcast(I32),
+                    )
 
         w_codes = []
         for w in range(3):
@@ -59,47 +64,28 @@ def tile_picked_maxout_max_e_kernel(
             )
             w_codes.append(codes)
 
-        w_scales = keep.tile([P, 3 * PASSES * N], U8, name="w_scales", align_bytes=64)
-        nc.gpsimd.memset(w_scales[:].bitcast(I32), 0)
-        for q in range(QUADS):
-            nc.gpsimd.dma_start(
-                out=w_scales[32 * q : 32 * q + 4, :].bitcast(I32),
-                in_=staged[4 * q : 4 * q + 4, :, :, :].rearrange("r w z n -> r (w z n)").bitcast(I32),
-            )
-
         x_codes, x_scales = {}, {}
         cols = HALF // 16
-
-        rows0 = keep.tile([P, PACK, S], BF16, name="rows0", align_bytes=64)
-        for t in range(PACK):
-            nc.vector.tensor_copy(out=rows0[:, t, :], in_=planes[0, t][:].indirect(offsets[:]))
         picked0 = keep.tile([P, S, PACK], BF16, name="picked0", align_bytes=64)
-        nc.scalar.copy(out=picked0[:], in_=rows0[:].rearrange("p t n -> p n t"))
+        picked1 = [keep.tile([P, HALF, PACK], BF16, name=f"picked1{h}", align_bytes=64) for h in range(HALVES)]
         codes0 = keep.tile([P, S], U32, name="codes0", align_bytes=64)
         scales0 = keep.tile([P, S], U8, name="scales0", align_bytes=64)
-        nc.vector.quantize_mx(
-            out=codes0[:].bitcast(FP8X4), scales=scales0[:], in_=picked0[:].rearrange("p n t -> p (n t)")
-        )
+        for z, t in ORDER:
+            if z == 0:
+                nc.vector.tensor_copy(out=picked0[:, :, t], in_=planes[z, t][:].indirect(offsets[:]))
+            else:
+                for h in range(HALVES):
+                    nc.vector.tensor_copy(
+                        out=picked1[h][:, :, t],
+                        in_=planes[z, t][:].indirect(offsets[:, h * cols : (h + 1) * cols]),
+                    )
+            if (z, t) == (0, PACK - 1):
+                nc.vector.quantize_mx(
+                    out=codes0[:].bitcast(FP8X4), scales=scales0[:], in_=picked0[:].rearrange("p n t -> p (n t)")
+                )
         for h in range(HALVES):
             x_codes[0, h] = codes0[:, h * HALF : (h + 1) * HALF]
             x_scales[0, h] = scales0[:, h * HALF : (h + 1) * HALF]
-
-        rows1 = keep.tile([P, 2, S], BF16, name="rows1", align_bytes=64)
-        for t in range(2):
-            nc.vector.tensor_copy(out=rows1[:, t, :], in_=planes[1, t][:].indirect(offsets[:]))
-        picked1 = [keep.tile([P, HALF, PACK], BF16, name=f"picked1{h}", align_bytes=64) for h in range(HALVES)]
-        for h in range(HALVES):
-            nc.scalar.copy(
-                out=picked1[h][:, :, 0:2],
-                in_=rows1[:, :, h * HALF : (h + 1) * HALF].rearrange("p t n -> p n t"),
-            )
-        for t in range(2, PACK):
-            for h in range(HALVES):
-                nc.vector.tensor_copy(
-                    out=picked1[h][:, :, t],
-                    in_=planes[1, t][:].indirect(offsets[:, h * cols : (h + 1) * cols]),
-                )
-        for h in range(HALVES):
             codes1 = keep.tile([P, HALF], U32, name=f"codes1{h}", align_bytes=64)
             scales1 = keep.tile([P, HALF], U8, name=f"scales1{h}", align_bytes=64)
             nc.vector.quantize_mx(
@@ -108,33 +94,58 @@ def tile_picked_maxout_max_e_kernel(
             x_codes[1, h] = codes1[:]
             x_scales[1, h] = scales1[:]
 
-        for h in range(HALVES):
-            acc = {}
-            for w in range(3):
-                for m in range(M_TILES):
-                    acc[w, m] = psum.tile([P, HALF], F32, name="acc")
-            for z in range(PASSES):
-                for w in range(3):
-                    for m in range(M_TILES):
-                        rows = slice(m * P, (m + 1) * P)
-                        first_byte = (w * PASSES + z) * N + m * P
-                        nc.tensor.matmul_mx(
-                            out=acc[w, m][:],
-                            lhsT=w_codes[w][:, z, rows].bitcast(FP8X4),
-                            lhsT_scale=w_scales[:, first_byte : first_byte + P],
-                            rhs=x_codes[z, h].bitcast(FP8X4),
-                            rhs_scale=x_scales[z, h],
-                            start=(z == 0),
-                            stop=(z == PASSES - 1),
-                        )
+        warm = psum.tile([P, S], F32, name="acc")
+        for i in range(WARM):
+            nc.tensor.matmul_mx(
+                out=warm[:],
+                lhsT=codes0[:, 0:P].bitcast(FP8X4),
+                lhsT_scale=scales0[:, 0:P],
+                rhs=codes0[:].bitcast(FP8X4),
+                rhs_scale=scales0[:],
+                start=True,
+                stop=True,
+            )
+
+        acc = {}
+
+        def product(h, w, m, z):
+            if z == 0:
+                acc[h, w, m] = psum.tile([P, HALF], F32, name="acc")
+            rows = slice(m * P, (m + 1) * P)
+            nc.tensor.matmul_mx(
+                out=acc[h, w, m][:],
+                lhsT=w_codes[w][:, z, rows].bitcast(FP8X4),
+                lhsT_scale=w_scales[4 * w : P, z, rows],
+                rhs=x_codes[z, h].bitcast(FP8X4),
+                rhs_scale=x_scales[z, h],
+                start=(z == 0),
+                stop=(z == PASSES - 1),
+            )
+
+        def largest(h):
             first, two, three = {}, {}, {}
             for m in range(M_TILES):
                 first[m] = keep.tile([P, HALF], F32, name=f"first{h}{m}")
-                nc.scalar.copy(out=first[m][:], in_=acc[0, m][:])
+                nc.scalar.copy(out=first[m][:], in_=acc[h, 0, m][:])
             for m in range(M_TILES):
                 two[m] = keep.tile([P, HALF], F32, name=f"two{h}{m}")
-                nc.vector.tensor_tensor(two[m][:], acc[1, m][:], first[m][:], MAX)
+                nc.vector.tensor_tensor(two[m][:], acc[h, 1, m][:], first[m][:], MAX)
             for m in range(M_TILES):
                 three[m] = keep.tile([P, HALF], F32, name=f"three{h}{m}")
-                nc.vector.tensor_tensor(three[m][:], acc[2, m][:], two[m][:], MAX)
+                nc.vector.tensor_tensor(three[m][:], acc[h, 2, m][:], two[m][:], MAX)
                 nc.sync.dma_start(out=out[m * P : (m + 1) * P, h * HALF : (h + 1) * HALF], in_=three[m][:])
+
+        groups = [(w, m) for w in range(3) for m in range(M_TILES)]
+        for w, m in groups:
+            product(0, w, m, 0)
+        for w, m in groups[:2]:
+            product(1, w, m, 0)
+        for w, m in groups:
+            product(0, w, m, 1)
+        largest(0)
+        for w, m in groups[:2]:
+            product(1, w, m, 1)
+        for w, m in groups[2:]:
+            product(1, w, m, 0)
+            product(1, w, m, 1)
+        largest(1)

@@ -40,13 +40,15 @@ def tile_picked_maxout_max_e_kernel(
         offsets = keep.tile([P, S // 16], U16, name="offsets")
         w_scales = keep.tile([P, PASSES, N], U8, name="w_scales", align_bytes=64)
         nc.vector.memset(w_scales[:].bitcast(I32), 0)
+        w3_rows = keep.tile([P, PASSES, N], U8, name="w3_rows", align_bytes=64)
+        nc.vector.memset(w3_rows[:].bitcast(I32), 0)
         planes = {}
         for i, (z, t) in enumerate(ORDER):
             planes[z, t] = keep.tile([P, T], F32, name=f"plane{z}{t}", align_bytes=64)
             nc.sync.dma_start(out=planes[z, t][:], in_=x_rows[z, t])
             if (z, t) == ORDER[0]:
                 nc.sync.dma_start(offsets[:], offs)
-            if 2 <= i < 5:
+            if 2 <= i < 4:
                 w = i - 2
                 for q in range(QUADS):
                     row = 32 * q + 4 * w
@@ -57,6 +59,12 @@ def tile_picked_maxout_max_e_kernel(
 
         w_codes = []
         for w in range(3):
+            if w == 2:
+                for q in range(QUADS):
+                    nc.sync.dma_start(
+                        out=w3_rows[32 * q : 32 * q + 4, :, :].bitcast(I32),
+                        in_=scales_in[w][:, 4 * q : 4 * q + 4, :].rearrange("z r n -> r z n").bitcast(I32),
+                    )
             codes = keep.tile([P, PASSES, N], U32, name=f"w_codes{w}", align_bytes=64)
             nc.sync.dma_start(
                 out=codes[:].bitcast(I32),
@@ -115,7 +123,7 @@ def tile_picked_maxout_max_e_kernel(
             nc.tensor.matmul_mx(
                 out=acc[h, w, m][:],
                 lhsT=w_codes[w][:, z, rows].bitcast(FP8X4),
-                lhsT_scale=w_scales[4 * w : P, z, rows],
+                lhsT_scale=w3_rows[:, z, rows] if w == 2 else w_scales[4 * w : P, z, rows],
                 rhs=x_codes[z, h].bitcast(FP8X4),
                 rhs_scale=x_scales[z, h],
                 start=(z == 0),
@@ -135,17 +143,22 @@ def tile_picked_maxout_max_e_kernel(
                 nc.vector.tensor_tensor(three[m][:], acc[h, 2, m][:], two[m][:], MAX)
                 nc.sync.dma_start(out=out[m * P : (m + 1) * P, h * HALF : (h + 1) * HALF], in_=three[m][:])
 
-        groups = [(w, m) for w in range(3) for m in range(M_TILES)]
-        for w, m in groups:
-            product(0, w, m, 0)
-        for w, m in groups[:2]:
-            product(1, w, m, 0)
-        for w, m in groups:
-            product(0, w, m, 1)
+        for h in range(HALVES):
+            for m in range(M_TILES):
+                product(h, 0, m, 0)
+        for m in range(M_TILES):
+            product(0, 1, m, 0)
+        for w in range(2):
+            for m in range(M_TILES):
+                product(0, w, m, 1)
+        for m in range(M_TILES):
+            product(0, 2, m, 0)
+            product(0, 2, m, 1)
         largest(0)
-        for w, m in groups[:2]:
-            product(1, w, m, 1)
-        for w, m in groups[2:]:
-            product(1, w, m, 0)
-            product(1, w, m, 1)
+        for m in range(M_TILES):
+            product(1, 0, m, 1)
+        for w in range(1, 3):
+            for m in range(M_TILES):
+                product(1, w, m, 0)
+                product(1, w, m, 1)
         largest(1)

@@ -21,7 +21,7 @@ HALVES = 2
 HALF = S // HALVES
 M_TILES = N // P
 QUADS = 4
-WARM = 3
+WARM = 6
 ORDER = [(0, 0), (0, 1), (0, 2), (1, 0), (1, 1), (0, 3), (1, 2), (1, 3)]
 
 
@@ -35,7 +35,7 @@ def tile_picked_maxout_max_e_kernel(
 
     with ExitStack() as ctx:
         keep = ctx.enter_context(tc.tile_pool(name="keep", bufs=1))
-        psum = ctx.enter_context(tc.psum_pool(name="psum", bufs=8))
+        psum = ctx.enter_context(tc.psum_pool(name="psum", bufs=1))
 
         offsets = keep.tile([P, S // 16], U16, name="offsets")
         w_scales = keep.tile([P, PASSES, N], U8, name="w_scales", align_bytes=64)
@@ -74,42 +74,42 @@ def tile_picked_maxout_max_e_kernel(
 
         x_codes, x_scales = {}, {}
         cols = HALF // 16
-        picked0 = keep.tile([P, S, PACK], BF16, name="picked0", align_bytes=64)
-        picked1 = [keep.tile([P, HALF, PACK], BF16, name=f"picked1{h}", align_bytes=64) for h in range(HALVES)]
-        codes0 = keep.tile([P, S], U32, name="codes0", align_bytes=64)
-        scales0 = keep.tile([P, S], U8, name="scales0", align_bytes=64)
+        pairs = [keep.tile([P, 2, S, 2], BF16, name=f"pairs{z}", align_bytes=64) for z in range(PASSES)]
         for z, t in ORDER:
-            if z == 0:
-                nc.vector.tensor_copy(out=picked0[:, :, t], in_=planes[z, t][:].indirect(offsets[:]))
-            else:
-                for h in range(HALVES):
-                    nc.vector.tensor_copy(
-                        out=picked1[h][:, :, t],
-                        in_=planes[z, t][:].indirect(offsets[:, h * cols : (h + 1) * cols]),
-                    )
-            if (z, t) == (0, PACK - 1):
-                nc.vector.quantize_mx(
-                    out=codes0[:].bitcast(FP8X4), scales=scales0[:], in_=picked0[:].rearrange("p n t -> p (n t)")
+            if t < PACK - 1:
+                nc.vector.tensor_copy(out=pairs[z][:, t // 2, :, t % 2], in_=planes[z, t][:].indirect(offsets[:]))
+                continue
+            for h in range(HALVES):
+                nc.vector.tensor_copy(
+                    out=pairs[z][:, t // 2, h * HALF : (h + 1) * HALF, t % 2],
+                    in_=planes[z, t][:].indirect(offsets[:, h * cols : (h + 1) * cols]),
                 )
-        for h in range(HALVES):
-            x_codes[0, h] = codes0[:, h * HALF : (h + 1) * HALF]
-            x_scales[0, h] = scales0[:, h * HALF : (h + 1) * HALF]
-            codes1 = keep.tile([P, HALF], U32, name=f"codes1{h}", align_bytes=64)
-            scales1 = keep.tile([P, HALF], U8, name=f"scales1{h}", align_bytes=64)
-            nc.vector.quantize_mx(
-                out=codes1[:].bitcast(FP8X4), scales=scales1[:], in_=picked1[h][:].rearrange("p n t -> p (n t)")
-            )
-            x_codes[1, h] = codes1[:]
-            x_scales[1, h] = scales1[:]
+            words = pairs[z][:].rearrange("p u n e -> p (u n e)").bitcast(U32).rearrange("p (u n) -> p n u", u=2)
+            woven = {}
+            for h in range(HALVES):
+                if (z, h) == (0, 1):
+                    woven[h] = pairs[1][:, 1, :, :].rearrange("p n e -> p (n e)")
+                else:
+                    woven[h] = keep.tile([P, PACK * HALF], BF16, name=f"woven{z}{h}", align_bytes=64)[:]
+                nc.scalar.copy(
+                    out=woven[h].bitcast(U32).rearrange("p (n u) -> p n u", u=2),
+                    in_=words[:, h * HALF : (h + 1) * HALF, :],
+                )
+            for h in range(HALVES):
+                codes = keep.tile([P, HALF], U32, name=f"codes{z}{h}", align_bytes=64)
+                scales = keep.tile([P, HALF], U8, name=f"scales{z}{h}", align_bytes=64)
+                nc.vector.quantize_mx(out=codes[:].bitcast(FP8X4), scales=scales[:], in_=woven[h])
+                x_codes[z, h] = codes[:]
+                x_scales[z, h] = scales[:]
 
-        warm = psum.tile([P, S], F32, name="acc")
+        warm = psum.tile([P, HALF], F32, name="warm", tag="bank7")
         for i in range(WARM):
             nc.tensor.matmul_mx(
                 out=warm[:],
-                lhsT=codes0[:, 0:P].bitcast(FP8X4),
-                lhsT_scale=scales0[:, 0:P],
-                rhs=codes0[:].bitcast(FP8X4),
-                rhs_scale=scales0[:],
+                lhsT=x_codes[0, 1][:, 0:P].bitcast(FP8X4),
+                lhsT_scale=x_scales[0, 1][:, 0:P],
+                rhs=x_codes[0, 1].bitcast(FP8X4),
+                rhs_scale=x_scales[0, 1],
                 start=True,
                 stop=True,
             )
@@ -118,7 +118,8 @@ def tile_picked_maxout_max_e_kernel(
 
         def product(h, w, m, z):
             if z == 0:
-                acc[h, w, m] = psum.tile([P, HALF], F32, name="acc")
+                bank = 4 * (h if w == 2 else w) + 2 * (0 if w == 2 else h) + m
+                acc[h, w, m] = psum.tile([P, HALF], F32, name=f"acc{h}{w}{m}", tag=f"bank{bank}")
             rows = slice(m * P, (m + 1) * P)
             nc.tensor.matmul_mx(
                 out=acc[h, w, m][:],
@@ -130,35 +131,41 @@ def tile_picked_maxout_max_e_kernel(
                 stop=(z == PASSES - 1),
             )
 
-        def largest(h):
-            first, two, three = {}, {}, {}
-            for m in range(M_TILES):
-                first[m] = keep.tile([P, HALF], F32, name=f"first{h}{m}")
-                nc.scalar.copy(out=first[m][:], in_=acc[h, 0, m][:])
-            for m in range(M_TILES):
-                two[m] = keep.tile([P, HALF], F32, name=f"two{h}{m}")
-                nc.vector.tensor_tensor(two[m][:], acc[h, 1, m][:], first[m][:], MAX)
-            for m in range(M_TILES):
-                three[m] = keep.tile([P, HALF], F32, name=f"three{h}{m}")
-                nc.vector.tensor_tensor(three[m][:], acc[h, 2, m][:], two[m][:], MAX)
-                nc.sync.dma_start(out=out[m * P : (m + 1) * P, h * HALF : (h + 1) * HALF], in_=three[m][:])
+        first, two = {}, {}
 
-        for h in range(HALVES):
+        def take_first(h):
             for m in range(M_TILES):
-                product(h, 0, m, 0)
-        for m in range(M_TILES):
-            product(0, 1, m, 0)
+                first[h, m] = keep.tile([P, HALF], F32, name=f"first{h}{m}")
+                nc.scalar.copy(out=first[h, m][:], in_=acc[h, 0, m][:])
+
+        def larger_of_two(h):
+            for m in range(M_TILES):
+                two[h, m] = keep.tile([P, HALF], F32, name=f"two{h}{m}")
+                nc.vector.tensor_tensor(two[h, m][:], acc[h, 1, m][:], first[h, m][:], MAX)
+
+        def largest(h):
+            for m in range(M_TILES):
+                three = keep.tile([P, HALF], F32, name=f"three{h}{m}")
+                nc.vector.tensor_tensor(three[:], acc[h, 2, m][:], two[h, m][:], MAX)
+                nc.sync.dma_start(out=out[m * P : (m + 1) * P, h * HALF : (h + 1) * HALF], in_=three[:])
+
+        def products(h, w, passes):
+            for m in range(M_TILES):
+                for z in passes:
+                    product(h, w, m, z)
+
         for w in range(2):
-            for m in range(M_TILES):
-                product(0, w, m, 1)
-        for m in range(M_TILES):
-            product(0, 2, m, 0)
-            product(0, 2, m, 1)
+            for h in range(HALVES):
+                products(h, w, [0])
+        products(0, 0, [1])
+        products(0, 1, [1])
+        take_first(0)
+        larger_of_two(0)
+        products(1, 0, [1])
+        take_first(1)
+        products(0, 2, [0, 1])
         largest(0)
-        for m in range(M_TILES):
-            product(1, 0, m, 1)
-        for w in range(1, 3):
-            for m in range(M_TILES):
-                product(1, w, m, 0)
-                product(1, w, m, 1)
+        products(1, 1, [1])
+        larger_of_two(1)
+        products(1, 2, [0, 1])
         largest(1)

@@ -17,12 +17,17 @@ MAX = mybir.AluOpType.max
 P = 128
 PACK = 4
 PASSES = K // (P * PACK)
+WEIGHTS = 3
 HALVES = 2
 HALF = S // HALVES
 M_TILES = N // P
 QUADS = 4
-WARM = 6
-ORDER = [(0, 0), (0, 1), (0, 2), (1, 0), (1, 1), (0, 3), (1, 2), (1, 3)]
+SCALE_ROWS = 4
+LIST_ROWS = 16
+WARM_UPS = 2
+
+LOADS = [(0, 0, 2), (1, 0, 2), (0, 2, 1), (0, 3, 1), (1, 2, 1), (1, 3, 1)]
+SCALES_BEHIND_LOAD = {1: 0, 4: 1}
 
 
 def tile_picked_maxout_max_e_kernel(
@@ -31,141 +36,163 @@ def tile_picked_maxout_max_e_kernel(
     nc = tc.nc
     words_in = (w1_words, w2_words, w3_words)
     scales_in = (w1_scales, w2_scales, w3_scales)
-    x_rows = xT.rearrange("(z p t) n -> z t p n", z=PASSES, t=PACK)
+    x_rows = xT.rearrange("(z p t) n -> z p t n", z=PASSES, t=PACK)
 
     with ExitStack() as ctx:
         keep = ctx.enter_context(tc.tile_pool(name="keep", bufs=1))
         psum = ctx.enter_context(tc.psum_pool(name="psum", bufs=1))
 
-        offsets = keep.tile([P, S // 16], U16, name="offsets")
-        w_scales = keep.tile([P, PASSES, N], U8, name="w_scales", align_bytes=64)
-        nc.vector.memset(w_scales[:].bitcast(I32), 0)
-        w3_rows = keep.tile([P, PASSES, N], U8, name="w3_rows", align_bytes=64)
-        nc.vector.memset(w3_rows[:].bitcast(I32), 0)
-        planes = {}
-        for i, (z, t) in enumerate(ORDER):
-            planes[z, t] = keep.tile([P, T], F32, name=f"plane{z}{t}", align_bytes=64)
-            nc.sync.dma_start(out=planes[z, t][:], in_=x_rows[z, t])
-            if (z, t) == ORDER[0]:
-                nc.sync.dma_start(offsets[:], offs)
-            if 2 <= i < 4:
-                w = i - 2
-                for q in range(QUADS):
-                    row = 32 * q + 4 * w
-                    nc.sync.dma_start(
-                        out=w_scales[row : row + 4, :, :].bitcast(I32),
-                        in_=scales_in[w][:, 4 * q : 4 * q + 4, :].rearrange("z r n -> r z n").bitcast(I32),
-                    )
+        offsets = keep.tile([P, S // LIST_ROWS], U16, name="offsets")
+        w_scales, w_codes = [], []
+        for w in range(WEIGHTS):
+            w_scales.append(keep.tile([P, PASSES, N], U8, name=f"w_scales{w}", align_bytes=64))
+            nc.vector.memset(w_scales[w][:].bitcast(I32), 0)
+            w_codes.append(keep.tile([P, PASSES, N], U32, name=f"w_codes{w}", align_bytes=64))
 
-        w_codes = []
-        for w in range(3):
-            if w == 2:
-                for q in range(QUADS):
-                    nc.sync.dma_start(
-                        out=w3_rows[32 * q : 32 * q + 4, :, :].bitcast(I32),
-                        in_=scales_in[w][:, 4 * q : 4 * q + 4, :].rearrange("z r n -> r z n").bitcast(I32),
-                    )
-            codes = keep.tile([P, PASSES, N], U32, name=f"w_codes{w}", align_bytes=64)
+        def load_scales(w):
+            for q in range(QUADS):
+                row = 32 * q + SCALE_ROWS * w
+                nc.sync.dma_start(
+                    out=w_scales[w][row : row + SCALE_ROWS, :, :].bitcast(I32),
+                    in_=scales_in[w][:, SCALE_ROWS * q : SCALE_ROWS * (q + 1), :]
+                    .rearrange("z r n -> r z n")
+                    .bitcast(I32),
+                )
+
+        def load_words(w):
             nc.sync.dma_start(
-                out=codes[:].bitcast(I32),
+                out=w_codes[w][:].bitcast(I32),
                 in_=words_in[w].rearrange("z p n t -> p z (n t)").bitcast(I32),
             )
-            w_codes.append(codes)
 
-        x_codes, x_scales = {}, {}
-        cols = HALF // 16
-        pairs = [keep.tile([P, 2, S, 2], BF16, name=f"pairs{z}", align_bytes=64) for z in range(PASSES)]
-        for z, t in ORDER:
-            if t < PACK - 1:
-                nc.vector.tensor_copy(out=pairs[z][:, t // 2, :, t % 2], in_=planes[z, t][:].indirect(offsets[:]))
-                continue
-            for h in range(HALVES):
-                nc.vector.tensor_copy(
-                    out=pairs[z][:, t // 2, h * HALF : (h + 1) * HALF, t % 2],
-                    in_=planes[z, t][:].indirect(offsets[:, h * cols : (h + 1) * cols]),
-                )
-            words = pairs[z][:].rearrange("p u n e -> p (u n e)").bitcast(U32).rearrange("p (u n) -> p n u", u=2)
-            woven = {}
-            for h in range(HALVES):
-                if (z, h) == (0, 1):
-                    woven[h] = pairs[1][:, 1, :, :].rearrange("p n e -> p (n e)")
-                else:
-                    woven[h] = keep.tile([P, PACK * HALF], BF16, name=f"woven{z}{h}", align_bytes=64)[:]
+        planes = {}
+        for i, (z, t0, count) in enumerate(LOADS):
+            loaded = keep.tile([P, count, T], F32, name=f"rows{i}", align_bytes=64)
+            nc.sync.dma_start(out=loaded[:], in_=x_rows[z, :, t0 : t0 + count, :])
+            for t in range(count):
+                planes[z, t0 + t] = loaded[:, t, :]
+            if i == 0:
+                nc.sync.dma_start(offsets[:], offs)
+            if i in SCALES_BEHIND_LOAD:
+                load_scales(SCALES_BEHIND_LOAD[i])
+        load_words(0)
+        load_words(1)
+        load_scales(2)
+        load_words(2)
+
+        pairs = [
+            keep.tile([P, 2, S, 2], BF16, name="pairs0", align_bytes=64),
+            keep.tile([P, 2, S + HALF, 2], BF16, name="pairs1", align_bytes=64),
+        ]
+        x_codes, x_scales, woven = {}, {}, {}
+        for z in range(PASSES):
+            x_codes[z] = keep.tile([P, S], U32, name=f"codes{z}", align_bytes=64)
+            x_scales[z] = keep.tile([P, S], U8, name=f"scales{z}", align_bytes=64)
+        for h in range(HALVES):
+            start = 2 * S + h * PACK * HALF
+            woven[0, h] = pairs[1][:].rearrange("p u n e -> p (u n e)")[:, start : start + PACK * HALF]
+            woven[1, h] = keep.tile([P, PACK * HALF], BF16, name=f"woven{h}", align_bytes=64)[:]
+
+        def gather(z, t, first_entry, entries):
+            nc.vector.tensor_copy(
+                out=pairs[z][:, t // 2, first_entry : first_entry + entries, t % 2],
+                in_=planes[z, t].indirect(offsets[:, first_entry // LIST_ROWS : (first_entry + entries) // LIST_ROWS]),
+            )
+
+        def weave(z, h, piece):
+            pair_words = pairs[z][:].rearrange("p u n e -> p (u n e)").bitcast(U32).rearrange("p (u n) -> p n u", u=2)
+            for j in range(0, HALF, piece):
                 nc.scalar.copy(
-                    out=woven[h].bitcast(U32).rearrange("p (n u) -> p n u", u=2),
-                    in_=words[:, h * HALF : (h + 1) * HALF, :],
+                    out=woven[z, h][:, PACK * j : PACK * (j + piece)].bitcast(U32).rearrange("p (n u) -> p n u", u=2),
+                    in_=pair_words[:, h * HALF + j : h * HALF + j + piece, :],
                 )
-            for h in range(HALVES):
-                codes = keep.tile([P, HALF], U32, name=f"codes{z}{h}", align_bytes=64)
-                scales = keep.tile([P, HALF], U8, name=f"scales{z}{h}", align_bytes=64)
-                nc.vector.quantize_mx(out=codes[:].bitcast(FP8X4), scales=scales[:], in_=woven[h])
-                x_codes[z, h] = codes[:]
-                x_scales[z, h] = scales[:]
 
-        warm = psum.tile([P, HALF], F32, name="warm", tag="bank7")
-        for i in range(WARM):
+        def quantise(z, h, piece):
+            for j in range(0, HALF, piece):
+                entries = slice(h * HALF + j, h * HALF + j + piece)
+                nc.vector.quantize_mx(
+                    out=x_codes[z][:, entries].bitcast(FP8X4),
+                    scales=x_scales[z][:, entries],
+                    in_=woven[z, h][:, PACK * j : PACK * (j + piece)],
+                )
+
+        for z, t0, count in LOADS[:3]:
+            for t in range(t0, t0 + count):
+                gather(z, t, 0, S)
+        for h in range(HALVES):
+            gather(0, 3, h * HALF, HALF)
+        for h in range(HALVES):
+            weave(0, h, HALF)
+        for h in range(HALVES):
+            quantise(0, h, HALF)
+            gather(1, 2, h * HALF, HALF)
+        for h in range(HALVES):
+            gather(1, 3, h * HALF, HALF)
+        for h in range(HALVES):
+            weave(1, h, HALF // 2)
+        for h in range(HALVES):
+            quantise(1, h, HALF // 2)
+
+        warm = psum.tile([P, S], F32, name="warm", tag="bank7")
+        for i in range(WARM_UPS):
             nc.tensor.matmul_mx(
                 out=warm[:],
-                lhsT=x_codes[0, 1][:, 0:P].bitcast(FP8X4),
-                lhsT_scale=x_scales[0, 1][:, 0:P],
-                rhs=x_codes[0, 1].bitcast(FP8X4),
-                rhs_scale=x_scales[0, 1],
+                lhsT=x_codes[0][:, 0:P].bitcast(FP8X4),
+                lhsT_scale=x_scales[0][:, 0:P],
+                rhs=x_codes[0][:].bitcast(FP8X4),
+                rhs_scale=x_scales[0][:],
                 start=True,
                 stop=True,
             )
 
-        acc = {}
-
-        def product(h, w, m, z):
-            if z == 0:
-                bank = 4 * (h if w == 2 else w) + 2 * (0 if w == 2 else h) + m
-                acc[h, w, m] = psum.tile([P, HALF], F32, name=f"acc{h}{w}{m}", tag=f"bank{bank}")
-            rows = slice(m * P, (m + 1) * P)
-            nc.tensor.matmul_mx(
-                out=acc[h, w, m][:],
-                lhsT=w_codes[w][:, z, rows].bitcast(FP8X4),
-                lhsT_scale=w3_rows[:, z, rows] if w == 2 else w_scales[4 * w : P, z, rows],
-                rhs=x_codes[z, h].bitcast(FP8X4),
-                rhs_scale=x_scales[z, h],
-                start=(z == 0),
-                stop=(z == PASSES - 1),
-            )
-
-        first, two = {}, {}
-
-        def take_first(h):
-            for m in range(M_TILES):
-                first[h, m] = keep.tile([P, HALF], F32, name=f"first{h}{m}")
-                nc.scalar.copy(out=first[h, m][:], in_=acc[h, 0, m][:])
-
-        def larger_of_two(h):
-            for m in range(M_TILES):
-                two[h, m] = keep.tile([P, HALF], F32, name=f"two{h}{m}")
-                nc.vector.tensor_tensor(two[h, m][:], acc[h, 1, m][:], first[h, m][:], MAX)
-
-        def largest(h):
-            for m in range(M_TILES):
-                three = keep.tile([P, HALF], F32, name=f"three{h}{m}")
-                nc.vector.tensor_tensor(three[:], acc[h, 2, m][:], two[h, m][:], MAX)
-                nc.sync.dma_start(out=out[m * P : (m + 1) * P, h * HALF : (h + 1) * HALF], in_=three[:])
+        acc, of_w1, of_w12 = {}, {}, {}
 
         def products(h, w, passes):
             for m in range(M_TILES):
                 for z in passes:
-                    product(h, w, m, z)
+                    if z == 0:
+                        bank = 4 * h + m if w == 2 else 4 * w + 2 * h + m
+                        acc[h, w, m] = psum.tile([P, HALF], F32, name=f"acc{h}{w}{m}", tag=f"bank{bank}")
+                    out_rows = slice(m * P, (m + 1) * P)
+                    entries = slice(h * HALF, (h + 1) * HALF)
+                    nc.tensor.matmul_mx(
+                        out=acc[h, w, m][:],
+                        lhsT=w_codes[w][:, z, out_rows].bitcast(FP8X4),
+                        lhsT_scale=w_scales[w][SCALE_ROWS * w : P, z, out_rows],
+                        rhs=x_codes[z][:, entries].bitcast(FP8X4),
+                        rhs_scale=x_scales[z][:, entries],
+                        start=(z == 0),
+                        stop=(z == PASSES - 1),
+                    )
+
+        def copy_w1(h):
+            for m in range(M_TILES):
+                of_w1[h, m] = keep.tile([P, HALF], F32, name=f"first{h}{m}")
+                nc.scalar.copy(out=of_w1[h, m][:], in_=acc[h, 0, m][:])
+
+        def max_with_w2(h):
+            for m in range(M_TILES):
+                of_w12[h, m] = keep.tile([P, HALF], F32, name=f"two{h}{m}")
+                nc.vector.tensor_tensor(of_w12[h, m][:], acc[h, 1, m][:], of_w1[h, m][:], MAX)
+
+        def max_with_w3_and_store(h):
+            for m in range(M_TILES):
+                result = keep.tile([P, HALF], F32, name=f"three{h}{m}")
+                nc.vector.tensor_tensor(result[:], acc[h, 2, m][:], of_w12[h, m][:], MAX)
+                nc.sync.dma_start(out=out[m * P : (m + 1) * P, h * HALF : (h + 1) * HALF], in_=result[:])
 
         for w in range(2):
             for h in range(HALVES):
                 products(h, w, [0])
         products(0, 0, [1])
         products(0, 1, [1])
-        take_first(0)
-        larger_of_two(0)
+        copy_w1(0)
+        max_with_w2(0)
         products(1, 0, [1])
-        take_first(1)
+        copy_w1(1)
         products(0, 2, [0, 1])
-        largest(0)
+        max_with_w3_and_store(0)
         products(1, 1, [1])
-        larger_of_two(1)
+        max_with_w2(1)
         products(1, 2, [0, 1])
-        largest(1)
+        max_with_w3_and_store(1)

@@ -24,7 +24,9 @@ M_TILES = N // P
 QUADS = 4
 SCALE_ROWS = 4
 LIST_ROWS = 16
-WARM_UPS = 2
+PIECES = 4
+PIECE = S // PIECES
+WARM_UPS = 3
 
 LOADS = [(0, 0, 2), (1, 0, 2), (0, 2, 1), (0, 3, 1), (1, 2, 1), (1, 3, 1)]
 SCALES_BEHIND_LOAD = {1: 0, 4: 1}
@@ -80,18 +82,16 @@ def tile_picked_maxout_max_e_kernel(
         load_scales(2)
         load_words(2)
 
-        pairs = [
-            keep.tile([P, 2, S, 2], BF16, name="pairs0", align_bytes=64),
-            keep.tile([P, 2, S + HALF, 2], BF16, name="pairs1", align_bytes=64),
-        ]
+        pairs = [keep.tile([P, 2, S, 2], BF16, name=f"pairs{z}", align_bytes=64) for z in range(PASSES)]
         x_codes, x_scales, woven = {}, {}, {}
         for z in range(PASSES):
             x_codes[z] = keep.tile([P, S], U32, name=f"codes{z}", align_bytes=64)
             x_scales[z] = keep.tile([P, S], U8, name=f"scales{z}", align_bytes=64)
-        for h in range(HALVES):
-            start = 2 * S + h * PACK * HALF
-            woven[0, h] = pairs[1][:].rearrange("p u n e -> p (u n e)")[:, start : start + PACK * HALF]
-            woven[1, h] = keep.tile([P, PACK * HALF], BF16, name=f"woven{h}", align_bytes=64)[:]
+            for h in range(HALVES):
+                if (z, h) == (0, 1):
+                    woven[z, h] = pairs[1][:, 1, :, :].rearrange("p n e -> p (n e)")
+                else:
+                    woven[z, h] = keep.tile([P, PACK * HALF], BF16, name=f"woven{z}{h}", align_bytes=64)[:]
 
         def gather(z, t, first_entry, entries):
             nc.vector.tensor_copy(
@@ -122,10 +122,10 @@ def tile_picked_maxout_max_e_kernel(
         for h in range(HALVES):
             gather(0, 3, h * HALF, HALF)
         for h in range(HALVES):
-            weave(0, h, HALF)
+            weave(0, h, HALF // 2)
         for h in range(HALVES):
-            quantise(0, h, HALF)
-            gather(1, 2, h * HALF, HALF)
+            quantise(0, h, HALF // 2)
+        gather(1, 2, 0, S)
         for h in range(HALVES):
             gather(1, 3, h * HALF, HALF)
         for h in range(HALVES):
@@ -145,54 +145,55 @@ def tile_picked_maxout_max_e_kernel(
                 stop=True,
             )
 
-        acc, of_w1, of_w12 = {}, {}, {}
+        tiles = range(M_TILES)
 
-        def products(h, w, passes):
-            for m in range(M_TILES):
-                for z in passes:
-                    if z == 0:
-                        bank = 4 * h + m if w == 2 else 4 * w + 2 * h + m
-                        acc[h, w, m] = psum.tile([P, HALF], F32, name=f"acc{h}{w}{m}", tag=f"bank{bank}")
-                    out_rows = slice(m * P, (m + 1) * P)
-                    entries = slice(h * HALF, (h + 1) * HALF)
-                    nc.tensor.matmul_mx(
-                        out=acc[h, w, m][:],
-                        lhsT=w_codes[w][:, z, out_rows].bitcast(FP8X4),
-                        lhsT_scale=w_scales[w][SCALE_ROWS * w : P, z, out_rows],
-                        rhs=x_codes[z][:, entries].bitcast(FP8X4),
-                        rhs_scale=x_scales[z][:, entries],
-                        start=(z == 0),
-                        stop=(z == PASSES - 1),
-                    )
+        def one_pass(acc, w, m, z, entries, start, stop):
+            out_rows = slice(m * P, (m + 1) * P)
+            nc.tensor.matmul_mx(
+                out=acc,
+                lhsT=w_codes[w][:, z, out_rows].bitcast(FP8X4),
+                lhsT_scale=w_scales[w][SCALE_ROWS * w : P, z, out_rows],
+                rhs=x_codes[z][:, entries].bitcast(FP8X4),
+                rhs_scale=x_scales[z][:, entries],
+                start=start,
+                stop=stop,
+            )
 
-        def copy_w1(h):
-            for m in range(M_TILES):
-                of_w1[h, m] = keep.tile([P, HALF], F32, name=f"first{h}{m}")
-                nc.scalar.copy(out=of_w1[h, m][:], in_=acc[h, 0, m][:])
+        acc = {}
 
-        def max_with_w2(h):
-            for m in range(M_TILES):
-                of_w12[h, m] = keep.tile([P, HALF], F32, name=f"two{h}{m}")
-                nc.vector.tensor_tensor(of_w12[h, m][:], acc[h, 1, m][:], of_w1[h, m][:], MAX)
+        def piece_pass(w, c, z):
+            if z == 0:
+                acc[w, c] = psum.tile([P, M_TILES, PIECE], F32, name=f"acc{w}{c}", tag=f"bank{PIECES * w + c}")
+            for m in tiles:
+                one_pass(
+                    acc[w, c][:, m, :], w, m, z, slice(c * PIECE, (c + 1) * PIECE),
+                    start=(z == 0 and m == 0), stop=(z == PASSES - 1 and m == M_TILES - 1),
+                )
 
-        def max_with_w3_and_store(h):
-            for m in range(M_TILES):
+        of_w12 = [keep.tile([P, M_TILES, HALF], F32, name=f"two{h}") for h in range(HALVES)]
+
+        def first_max(c):
+            of_w1 = keep.tile([P, M_TILES, PIECE], F32, name=f"first{c}")
+            nc.scalar.copy(out=of_w1[:], in_=acc[0, c][:])
+            h, j = divmod(c * PIECE, HALF)
+            nc.vector.tensor_tensor(of_w12[h][:, :, j : j + PIECE], acc[1, c][:], of_w1[:], MAX)
+
+        for c in range(PIECES):
+            piece_pass(0, c, 0)
+        for c in range(PIECES - 1):
+            piece_pass(1, c, 0)
+        for c in range(PIECES):
+            piece_pass(0, c, 1)
+            if c == PIECES - 1:
+                piece_pass(1, c, 0)
+            piece_pass(1, c, 1)
+            first_max(c)
+        for h in range(HALVES):
+            entries = slice(h * HALF, (h + 1) * HALF)
+            for m in tiles:
+                of_w3 = psum.tile([P, HALF], F32, name=f"third{h}{m}", tag=f"bank{M_TILES * h + m}")
+                for z in range(PASSES):
+                    one_pass(of_w3[:], 2, m, z, entries, start=(z == 0), stop=(z == PASSES - 1))
                 result = keep.tile([P, HALF], F32, name=f"three{h}{m}")
-                nc.vector.tensor_tensor(result[:], acc[h, 2, m][:], of_w12[h, m][:], MAX)
-                nc.sync.dma_start(out=out[m * P : (m + 1) * P, h * HALF : (h + 1) * HALF], in_=result[:])
-
-        for w in range(2):
-            for h in range(HALVES):
-                products(h, w, [0])
-        products(0, 0, [1])
-        products(0, 1, [1])
-        copy_w1(0)
-        max_with_w2(0)
-        products(1, 0, [1])
-        copy_w1(1)
-        products(0, 2, [0, 1])
-        max_with_w3_and_store(0)
-        products(1, 1, [1])
-        max_with_w2(1)
-        products(1, 2, [0, 1])
-        max_with_w3_and_store(1)
+                nc.vector.tensor_tensor(result[:], of_w3[:], of_w12[h][:, m, :], MAX)
+                nc.sync.dma_start(out=out[m * P : (m + 1) * P, entries], in_=result[:])

@@ -51,8 +51,8 @@ def tile_picked_maxout_max_e_kernel(
             nc.vector.memset(w_scales[w][:].bitcast(I32), 0)
             w_codes.append(keep.tile([P, PASSES, N], U32, name=f"w_codes{w}", align_bytes=64))
 
-        def load_scales(w):
-            for q in range(QUADS):
+        def load_scales(w, quads=range(QUADS)):
+            for q in quads:
                 row = 32 * q + SCALE_ROWS * w
                 nc.sync.dma_start(
                     out=w_scales[w][row : row + SCALE_ROWS, :, :].bitcast(I32),
@@ -61,10 +61,10 @@ def tile_picked_maxout_max_e_kernel(
                     .bitcast(I32),
                 )
 
-        def load_words(w):
+        def load_words(w, passes=slice(0, PASSES)):
             nc.sync.dma_start(
-                out=w_codes[w][:].bitcast(I32),
-                in_=words_in[w].rearrange("z p n t -> p z (n t)").bitcast(I32),
+                out=w_codes[w][:, passes, :].bitcast(I32),
+                in_=words_in[w][passes].rearrange("z p n t -> p z (n t)").bitcast(I32),
             )
 
         planes = {}
@@ -77,10 +77,12 @@ def tile_picked_maxout_max_e_kernel(
                 nc.sync.dma_start(offsets[:], offs)
             if i in SCALES_BEHIND_LOAD:
                 load_scales(SCALES_BEHIND_LOAD[i])
-        load_words(0)
+        load_words(0, slice(0, 1))
         load_words(1)
-        load_scales(2)
+        load_words(0, slice(1, 2))
+        load_scales(2, range(QUADS - 1))
         load_words(2)
+        load_scales(2, [QUADS - 1])
 
         pairs = [keep.tile([P, 2, S, 2], BF16, name=f"pairs{z}", align_bytes=64) for z in range(PASSES)]
         x_codes, x_scales, woven = {}, {}, {}
@@ -180,12 +182,10 @@ def tile_picked_maxout_max_e_kernel(
 
         for c in range(PIECES):
             piece_pass(0, c, 0)
-        for c in range(PIECES - 1):
+        for c in range(PIECES):
             piece_pass(1, c, 0)
         for c in range(PIECES):
             piece_pass(0, c, 1)
-            if c == PIECES - 1:
-                piece_pass(1, c, 0)
             piece_pass(1, c, 1)
             first_max(c)
         for h in range(HALVES):

@@ -26,7 +26,7 @@ SCALE_ROWS = 4
 LIST_ROWS = 16
 PIECES = 4
 PIECE = S // PIECES
-WARM_UPS = 3
+WARM_UPS = 2 * [slice(PIECE, PIECE + HALF)] + 2 * [slice(0, S)]
 
 LOADS = [(0, 0, 2), (1, 0, 2), (0, 2, 1), (0, 3, 1), (1, 2, 1), (1, 3, 1)]
 SCALES_BEHIND_LOAD = {1: 0, 4: 1}
@@ -51,14 +51,12 @@ def tile_picked_maxout_max_e_kernel(
             nc.vector.memset(w_scales[w][:].bitcast(I32), 0)
             w_codes.append(keep.tile([P, PASSES, N], U32, name=f"w_codes{w}", align_bytes=64))
 
-        def load_scales(w, quads=range(QUADS)):
-            for q in quads:
-                row = 32 * q + SCALE_ROWS * w
+        def load_scales(w, rows=range(SCALE_ROWS)):
+            by_row = scales_in[w].rearrange("z (q r) n -> r q z n", r=SCALE_ROWS)
+            for r in rows:
                 nc.sync.dma_start(
-                    out=w_scales[w][row : row + SCALE_ROWS, :, :].bitcast(I32),
-                    in_=scales_in[w][:, SCALE_ROWS * q : SCALE_ROWS * (q + 1), :]
-                    .rearrange("z r n -> r z n")
-                    .bitcast(I32),
+                    out=w_scales[w][SCALE_ROWS * w + r : P : P // QUADS, :, :].bitcast(I32),
+                    in_=by_row[r].bitcast(I32),
                 )
 
         def load_words(w, passes=slice(0, PASSES)):
@@ -136,13 +134,13 @@ def tile_picked_maxout_max_e_kernel(
             quantise(1, h, HALF // 2)
 
         warm = psum.tile([P, S], F32, name="warm", tag="bank7")
-        for i in range(WARM_UPS):
+        for entries in WARM_UPS:
             nc.tensor.matmul_mx(
-                out=warm[:],
+                out=warm[:, entries],
                 lhsT=x_codes[0][:, 0:P].bitcast(FP8X4),
                 lhsT_scale=x_scales[0][:, 0:P],
-                rhs=x_codes[0][:].bitcast(FP8X4),
-                rhs_scale=x_scales[0][:],
+                rhs=x_codes[0][:, entries].bitcast(FP8X4),
+                rhs_scale=x_scales[0][:, entries],
                 start=True,
                 stop=True,
             )

@@ -26,10 +26,10 @@ SCALE_ROWS = 4
 LIST_ROWS = 16
 PIECES = 4
 PIECE = S // PIECES
-WARM_UPS = 2 * [slice(PIECE, PIECE + HALF)] + 2 * [slice(0, S)]
+WARM_UPS = 2 * [slice(0, HALF)] + 2 * [slice(0, S)]
 
 LOADS = [(0, 0, 2), (1, 0, 2), (0, 2, 1), (0, 3, 1), (1, 2, 1), (1, 3, 1)]
-SCALES_BEHIND_LOAD = {1: 0, 4: 1}
+SCALES_BEHIND_LOAD = {1: 0}
 
 
 def tile_picked_maxout_max_e_kernel(
@@ -76,11 +76,11 @@ def tile_picked_maxout_max_e_kernel(
             if i in SCALES_BEHIND_LOAD:
                 load_scales(SCALES_BEHIND_LOAD[i])
         load_words(0, slice(0, 1))
+        load_scales(1)
         load_words(1)
         load_words(0, slice(1, 2))
-        load_scales(2, range(QUADS - 1))
         load_words(2)
-        load_scales(2, [QUADS - 1])
+        load_scales(2)
 
         pairs = [keep.tile([P, 2, S, 2], BF16, name=f"pairs{z}", align_bytes=64) for z in range(PASSES)]
         x_codes, x_scales, woven = {}, {}, {}
@@ -180,10 +180,12 @@ def tile_picked_maxout_max_e_kernel(
 
         for c in range(PIECES):
             piece_pass(0, c, 0)
-        for c in range(PIECES):
+        for c in range(PIECES - 1):
             piece_pass(1, c, 0)
         for c in range(PIECES):
             piece_pass(0, c, 1)
+            if c == PIECES - 1:
+                piece_pass(1, c, 0)
             piece_pass(1, c, 1)
             first_max(c)
         for h in range(HALVES):

@@ -12,6 +12,7 @@ U32 = mybir.dt.uint32
 U16 = mybir.dt.uint16
 U8 = mybir.dt.uint8
 FP8X4 = mybir.dt.float8_e4m3fn_x4
+COPY = mybir.ActivationFunctionType.Copy
 MAX = mybir.AluOpType.max
 
 P = 128
@@ -26,10 +27,10 @@ SCALE_ROWS = 4
 LIST_ROWS = 16
 PIECES = 4
 PIECE = S // PIECES
-WARM_UPS = 2 * [slice(0, HALF)] + 2 * [slice(0, S)]
+WARM_UPS = [slice(0, S)]
 
 LOADS = [(0, 0, 2), (1, 0, 2), (0, 2, 1), (0, 3, 1), (1, 2, 1), (1, 3, 1)]
-SCALES_BEHIND_LOAD = {1: 0}
+SCALES_BEHIND_LOAD = {1: 0, 3: 1}
 
 
 def tile_picked_maxout_max_e_kernel(
@@ -46,9 +47,10 @@ def tile_picked_maxout_max_e_kernel(
 
         offsets = keep.tile([P, S // LIST_ROWS], U16, name="offsets")
         w_scales, w_codes = [], []
+        packed = keep.tile([P, 4, N], U8, name="packed", align_bytes=64)
+        nc.vector.memset(packed[:].bitcast(I32), 0)
+        w_scales = [packed[:, 0:4:2, :], packed[:, 1:4:2, :], packed[:, 2:4, :]]
         for w in range(WEIGHTS):
-            w_scales.append(keep.tile([P, PASSES, N], U8, name=f"w_scales{w}", align_bytes=64))
-            nc.vector.memset(w_scales[w][:].bitcast(I32), 0)
             w_codes.append(keep.tile([P, PASSES, N], U32, name=f"w_codes{w}", align_bytes=64))
 
         def load_scales(w, rows=range(SCALE_ROWS)):
@@ -67,20 +69,21 @@ def tile_picked_maxout_max_e_kernel(
 
         planes = {}
         for i, (z, t0, count) in enumerate(LOADS):
-            loaded = keep.tile([P, count, T], F32, name=f"rows{i}", align_bytes=64)
-            nc.sync.dma_start(out=loaded[:], in_=x_rows[z, :, t0 : t0 + count, :])
+            if i == len(LOADS) - 1:
+                load_words(0, slice(0, 1))
+            loaded = keep.tile([P, count * T], F32, name=f"rows{i}", align_bytes=64)
+            nc.sync.dma_start(out=loaded[:], in_=x_rows[z, :, t0 : t0 + count, :].rearrange("p t n -> p (t n)"))
             for t in range(count):
-                planes[z, t0 + t] = loaded[:, t, :]
+                planes[z, t0 + t] = loaded[:, t * T : (t + 1) * T]
             if i == 0:
                 nc.sync.dma_start(offsets[:], offs)
             if i in SCALES_BEHIND_LOAD:
                 load_scales(SCALES_BEHIND_LOAD[i])
-        load_words(0, slice(0, 1))
-        load_scales(1)
-        load_words(1)
+        load_words(1, slice(0, 1))
         load_words(0, slice(1, 2))
-        load_words(2)
+        load_words(1, slice(1, 2))
         load_scales(2)
+        load_words(2)
 
         pairs = [keep.tile([P, 2, S, 2], BF16, name=f"pairs{z}", align_bytes=64) for z in range(PASSES)]
         x_codes, x_scales, woven = {}, {}, {}
@@ -125,25 +128,26 @@ def tile_picked_maxout_max_e_kernel(
             weave(0, h, HALF // 2)
         for h in range(HALVES):
             quantise(0, h, HALF // 2)
-        gather(1, 2, 0, S)
         for h in range(HALVES):
-            gather(1, 3, h * HALF, HALF)
+            gather(1, 2, h * HALF, HALF)
         for h in range(HALVES):
-            weave(1, h, HALF // 2)
+            weave(1, h, HALF)
+
+        def last_slot(h):
+            return woven[1, h].rearrange("p (n t) -> p n t", t=PACK)[:, :, PACK - 1]
+
+        def listed(first_entry, entries):
+            return planes[1, 3].indirect(offsets[:, first_entry // LIST_ROWS : (first_entry + entries) // LIST_ROWS])
+
+        nc.vector.tensor_copy(out=last_slot(0), in_=listed(0, HALF))
+        dense = [keep.tile([P, PIECE], BF16, name=f"dense{j}", align_bytes=64) for j in range(2)]
+        for j in range(2):
+            nc.scalar.activation(out=dense[j][:], in_=listed(HALF + j * PIECE, PIECE), func=COPY)
+        for j in range(2):
+            nc.scalar.copy(out=last_slot(1)[:, j * PIECE : (j + 1) * PIECE], in_=dense[j][:])
         for h in range(HALVES):
             quantise(1, h, HALF // 2)
 
-        warm = psum.tile([P, S], F32, name="warm", tag="bank7")
-        for entries in WARM_UPS:
-            nc.tensor.matmul_mx(
-                out=warm[:, entries],
-                lhsT=x_codes[0][:, 0:P].bitcast(FP8X4),
-                lhsT_scale=x_scales[0][:, 0:P],
-                rhs=x_codes[0][:, entries].bitcast(FP8X4),
-                rhs_scale=x_scales[0][:, entries],
-                start=True,
-                stop=True,
-            )
 
         tiles = range(M_TILES)
 
@@ -180,12 +184,13 @@ def tile_picked_maxout_max_e_kernel(
 
         for c in range(PIECES):
             piece_pass(0, c, 0)
-        for c in range(PIECES - 1):
+        warm = psum.tile([P, S], F32, name="warm", tag="bank7")
+        for entries in WARM_UPS:
+            one_pass(warm[:, entries], 0, 0, 0, entries, start=True, stop=True)
+        for c in range(PIECES):
             piece_pass(1, c, 0)
         for c in range(PIECES):
             piece_pass(0, c, 1)
-            if c == PIECES - 1:
-                piece_pass(1, c, 0)
             piece_pass(1, c, 1)
             first_max(c)
         for h in range(HALVES):

@@ -29,8 +29,8 @@ PIECES = 4
 PIECE = S // PIECES
 WARM_UPS = [slice(0, S)]
 
-LOADS = [(0, 0, 2), (1, 0, 2), (0, 2, 1), (0, 3, 1), (1, 2, 1), (1, 3, 1)]
-SCALES_BEHIND_LOAD = {1: 0, 3: 1}
+LOADS = [(0, 0, 4), (1, 0, 2), (1, 2, 1), (1, 3, 1)]
+SCALES_BEHIND_LOAD = {0: 0, 1: 1}
 
 
 def tile_picked_maxout_max_e_kernel(
@@ -48,7 +48,8 @@ def tile_picked_maxout_max_e_kernel(
         offsets = keep.tile([P, S // LIST_ROWS], U16, name="offsets")
         w_scales, w_codes = [], []
         packed = keep.tile([P, 4, N], U8, name="packed", align_bytes=64)
-        nc.vector.memset(packed[:].bitcast(I32), 0)
+        nc.vector.memset(packed[:, 0:2, :].bitcast(I32), 0)
+        nc.scalar.copy(out=packed[:, 2:4, :].bitcast(U32), in_=packed[:, 0:2, :].bitcast(U32))
         w_scales = [packed[:, 0:4:2, :], packed[:, 1:4:2, :], packed[:, 2:4, :]]
         for w in range(WEIGHTS):
             w_codes.append(keep.tile([P, PASSES, N], U32, name=f"w_codes{w}", align_bytes=64))
@@ -85,29 +86,33 @@ def tile_picked_maxout_max_e_kernel(
         load_scales(2)
         load_words(2)
 
-        pairs = [keep.tile([P, 2, S, 2], BF16, name=f"pairs{z}", align_bytes=64) for z in range(PASSES)]
+        pairs = {
+            (z, h): keep.tile([P, 2, HALF, 2], BF16, name=f"pairs{z}{h}", align_bytes=64)
+            for z in range(PASSES)
+            for h in range(HALVES)
+        }
         x_codes, x_scales, woven = {}, {}, {}
         for z in range(PASSES):
             x_codes[z] = keep.tile([P, S], U32, name=f"codes{z}", align_bytes=64)
             x_scales[z] = keep.tile([P, S], U8, name=f"scales{z}", align_bytes=64)
             for h in range(HALVES):
-                if (z, h) == (0, 1):
-                    woven[z, h] = pairs[1][:, 1, :, :].rearrange("p n e -> p (n e)")
+                if z == 0:
+                    woven[z, h] = pairs[1, h][:].rearrange("p u n e -> p (u n e)")
                 else:
                     woven[z, h] = keep.tile([P, PACK * HALF], BF16, name=f"woven{z}{h}", align_bytes=64)[:]
 
-        def gather(z, t, first_entry, entries):
+        def gather(z, t, h):
             nc.vector.tensor_copy(
-                out=pairs[z][:, t // 2, first_entry : first_entry + entries, t % 2],
-                in_=planes[z, t].indirect(offsets[:, first_entry // LIST_ROWS : (first_entry + entries) // LIST_ROWS]),
+                out=pairs[z, h][:, t // 2, :, t % 2],
+                in_=planes[z, t].indirect(offsets[:, h * HALF // LIST_ROWS : (h + 1) * HALF // LIST_ROWS]),
             )
 
         def weave(z, h, piece):
-            pair_words = pairs[z][:].rearrange("p u n e -> p (u n e)").bitcast(U32).rearrange("p (u n) -> p n u", u=2)
+            pair_words = pairs[z, h][:].rearrange("p u n e -> p (u n e)").bitcast(U32).rearrange("p (u n) -> p n u", u=2)
             for j in range(0, HALF, piece):
                 nc.scalar.copy(
                     out=woven[z, h][:, PACK * j : PACK * (j + piece)].bitcast(U32).rearrange("p (n u) -> p n u", u=2),
-                    in_=pair_words[:, h * HALF + j : h * HALF + j + piece, :],
+                    in_=pair_words[:, j : j + piece, :],
                 )
 
         def quantise(z, h, piece):
@@ -119,17 +124,24 @@ def tile_picked_maxout_max_e_kernel(
                     in_=woven[z, h][:, PACK * j : PACK * (j + piece)],
                 )
 
-        for z, t0, count in LOADS[:3]:
-            for t in range(t0, t0 + count):
-                gather(z, t, 0, S)
-        for h in range(HALVES):
-            gather(0, 3, h * HALF, HALF)
-        for h in range(HALVES):
-            weave(0, h, HALF // 2)
-        for h in range(HALVES):
-            quantise(0, h, HALF // 2)
-        for h in range(HALVES):
-            gather(1, 2, h * HALF, HALF)
+        def gather_on_scalar(z, u):
+            picked = keep.tile([P, 2, HALF], F32, name=f"picked{z}", align_bytes=64)
+            for e in range(2):
+                nc.scalar.activation(
+                    out=picked[:, e, :], in_=planes[z, 2 * u + e].indirect(offsets[:, HALF // LIST_ROWS :]), func=COPY
+                )
+            nc.scalar.copy(out=pairs[z, 1][:, u, :, :], in_=picked[:].rearrange("p e n -> p n e"))
+
+        gather_on_scalar(0, 1)
+        for t, h in [(0, 1), (0, 0), (1, 1), (1, 0), (2, 0), (3, 0)]:
+            gather(0, t, h)
+        for h in reversed(range(HALVES)):
+            weave(0, h, HALF)
+        for h in reversed(range(HALVES)):
+            quantise(0, h, HALF)
+        gather_on_scalar(1, 0)
+        for t, h in [(0, 0), (1, 0), (2, 0), (2, 1)]:
+            gather(1, t, h)
         for h in range(HALVES):
             weave(1, h, HALF)
 
@@ -140,11 +152,11 @@ def tile_picked_maxout_max_e_kernel(
             return planes[1, 3].indirect(offsets[:, first_entry // LIST_ROWS : (first_entry + entries) // LIST_ROWS])
 
         nc.vector.tensor_copy(out=last_slot(0), in_=listed(0, HALF))
-        dense = [keep.tile([P, PIECE], BF16, name=f"dense{j}", align_bytes=64) for j in range(2)]
+        dense = [keep.tile([P, PIECE], BF16, name=f"dense{j}", align_bytes=64)[:] for j in range(2)]
         for j in range(2):
-            nc.scalar.activation(out=dense[j][:], in_=listed(HALF + j * PIECE, PIECE), func=COPY)
+            nc.scalar.activation(out=dense[j], in_=listed(HALF + j * PIECE, PIECE), func=COPY)
         for j in range(2):
-            nc.scalar.copy(out=last_slot(1)[:, j * PIECE : (j + 1) * PIECE], in_=dense[j][:])
+            nc.scalar.copy(out=last_slot(1)[:, j * PIECE : (j + 1) * PIECE], in_=dense[j])
         for h in range(HALVES):
             quantise(1, h, HALF // 2)
 

@@ -14,6 +14,7 @@ U8 = mybir.dt.uint8
 FP8X4 = mybir.dt.float8_e4m3fn_x4
 COPY = mybir.ActivationFunctionType.Copy
 MAX = mybir.AluOpType.max
+AXIS_X = mybir.AxisListType.X
 
 P = 128
 PACK = 4
@@ -71,6 +72,7 @@ def tile_picked_maxout_max_e_kernel(
         planes = {}
         for i, (z, t0, count) in enumerate(LOADS):
             if i == len(LOADS) - 1:
+                load_scales(2, range(1))
                 load_words(0, slice(0, 1))
             loaded = keep.tile([P, count * T], F32, name=f"rows{i}", align_bytes=64)
             nc.sync.dma_start(out=loaded[:], in_=x_rows[z, :, t0 : t0 + count, :].rearrange("p t n -> p (t n)"))
@@ -83,7 +85,7 @@ def tile_picked_maxout_max_e_kernel(
         load_words(1, slice(0, 1))
         load_words(0, slice(1, 2))
         load_words(1, slice(1, 2))
-        load_scales(2)
+        load_scales(2, range(1, SCALE_ROWS))
         load_words(2)
 
         pairs = {
@@ -175,7 +177,11 @@ def tile_picked_maxout_max_e_kernel(
                 stop=stop,
             )
 
+        both = [psum.tile([P, 2, PIECE], F32, name=f"both{m}", tag=f"bank{PIECES * m}") for m in tiles]
         acc = {}
+
+        def first_piece_pass(w, m, z):
+            one_pass(both[m][:, w, :], w, m, z, slice(0, PIECE), start=(w, z) == (0, 0), stop=(w, z) == (1, 1))
 
         def piece_pass(w, c, z):
             if z == 0:
@@ -188,29 +194,53 @@ def tile_picked_maxout_max_e_kernel(
 
         of_w12 = [keep.tile([P, M_TILES, HALF], F32, name=f"two{h}") for h in range(HALVES)]
 
-        def first_max(c):
-            of_w1 = keep.tile([P, M_TILES, PIECE], F32, name=f"first{c}")
-            nc.scalar.copy(out=of_w1[:], in_=acc[0, c][:])
-            h, j = divmod(c * PIECE, HALF)
-            nc.vector.tensor_tensor(of_w12[h][:, :, j : j + PIECE], acc[1, c][:], of_w1[:], MAX)
+        def reduce_first_piece(m):
+            for w in range(2):
+                first_piece_pass(w, m, 1)
+            nc.vector.tensor_reduce(
+                out=of_w12[0][:, m, 0:PIECE], in_=both[m][:].rearrange("p w n -> p n w"), axis=AXIS_X, op=MAX
+            )
 
-        for c in range(PIECES):
-            piece_pass(0, c, 0)
+        of_w1 = {}
+
+        def w1_out(c):
+            piece_pass(0, c, 1)
+            of_w1[c] = keep.tile([P, M_TILES, PIECE], F32, name=f"first{c}")
+            nc.scalar.copy(out=of_w1[c][:], in_=acc[0, c][:])
+
+        def first_max(c):
+            piece_pass(1, c, 1)
+            h, j = divmod(c * PIECE, HALF)
+            nc.vector.tensor_tensor(of_w12[h][:, :, j : j + PIECE], acc[1, c][:], of_w1[c][:], MAX)
+
+        def finish(h, m, bank):
+            entries = slice(h * HALF, (h + 1) * HALF)
+            of_w3 = psum.tile([P, HALF], F32, name=f"third{h}{m}", tag=f"bank{bank}")
+            for z in range(PASSES):
+                one_pass(of_w3[:], 2, m, z, entries, start=(z == 0), stop=(z == PASSES - 1))
+            result = keep.tile([P, HALF], F32, name=f"three{h}{m}")
+            nc.vector.tensor_tensor(result[:], of_w3[:], of_w12[h][:, m, :], MAX)
+            nc.sync.dma_start(out=out[m * P : (m + 1) * P, entries], in_=result[:])
+
+        def opening_passes(w):
+            for m in tiles:
+                first_piece_pass(w, m, 0)
+            for c in range(1, PIECES):
+                piece_pass(w, c, 0)
+
+        opening_passes(0)
         warm = psum.tile([P, S], F32, name="warm", tag="bank7")
         for entries in WARM_UPS:
             one_pass(warm[:, entries], 0, 0, 0, entries, start=True, stop=True)
-        for c in range(PIECES):
-            piece_pass(1, c, 0)
-        for c in range(PIECES):
-            piece_pass(0, c, 1)
-            piece_pass(1, c, 1)
+        opening_passes(1)
+        reduce_first_piece(0)
+        w1_out(1)
+        reduce_first_piece(1)
+        for c in range(1, PIECES):
+            if c + 1 < PIECES:
+                w1_out(c + 1)
             first_max(c)
-        for h in range(HALVES):
-            entries = slice(h * HALF, (h + 1) * HALF)
-            for m in tiles:
-                of_w3 = psum.tile([P, HALF], F32, name=f"third{h}{m}", tag=f"bank{M_TILES * h + m}")
-                for z in range(PASSES):
-                    one_pass(of_w3[:], 2, m, z, entries, start=(z == 0), stop=(z == PASSES - 1))
-                result = keep.tile([P, HALF], F32, name=f"three{h}{m}")
-                nc.vector.tensor_tensor(result[:], of_w3[:], of_w12[h][:, m, :], MAX)
-                nc.sync.dma_start(out=out[m * P : (m + 1) * P, entries], in_=result[:])
+        finish(0, 0, 0)
+        finish(0, 1, PIECES)
+        finish(1, 0, 1)
+        finish(1, 1, 2)

@@ -31,7 +31,6 @@ PIECE = S // PIECES
 WARM_UPS = [slice(0, S)]
 
 LOADS = [(0, 0, 4), (1, 0, 2), (1, 2, 1), (1, 3, 1)]
-SCALES_BEHIND_LOAD = {0: 0, 1: 1}
 
 
 def tile_picked_maxout_max_e_kernel(
@@ -47,46 +46,47 @@ def tile_picked_maxout_max_e_kernel(
         psum = ctx.enter_context(tc.psum_pool(name="psum", bufs=1))
 
         offsets = keep.tile([P, S // LIST_ROWS], U16, name="offsets")
-        w_scales, w_codes = [], []
-        packed = keep.tile([P, 4, N], U8, name="packed", align_bytes=64)
-        nc.vector.memset(packed[:, 0:2, :].bitcast(I32), 0)
-        nc.scalar.copy(out=packed[:, 2:4, :].bitcast(U32), in_=packed[:, 0:2, :].bitcast(U32))
-        w_scales = [packed[:, 0:4:2, :], packed[:, 1:4:2, :], packed[:, 2:4, :]]
-        for w in range(WEIGHTS):
-            w_codes.append(keep.tile([P, PASSES, N], U32, name=f"w_codes{w}", align_bytes=64))
+        packed = keep.tile([P, 5, N], U8, name="packed", align_bytes=64)
+        nc.vector.memset(packed[:, 0:3, :].bitcast(I32), 0)
+        nc.scalar.copy(out=packed[:, 3:5, :].bitcast(U32), in_=packed[:, 0:2, :].bitcast(U32))
+        w_scales = [packed[:, 0:3:2, :], packed[:, 1:3, :], packed[:, 3:5, :]]
+        late = keep.tile([P, 2, PACK * N], U8, name="late", align_bytes=64)
+        first = [keep.tile([P, PACK * N], U8, name=f"first_words{w}", align_bytes=64) for w in range(2)]
+        third = keep.tile([P, PASSES, PACK * N], U8, name="third", align_bytes=64)
+        w_codes = {(w, 0): first[w][:] for w in range(2)}
+        w_codes.update({(w, 1): late[:, w, :] for w in range(2)})
+        w_codes.update({(2, z): third[:, z, :] for z in range(PASSES)})
 
-        def load_scales(w, rows=range(SCALE_ROWS)):
+        def load_scales(w, rows=range(SCALE_ROWS), passes=slice(0, PASSES)):
             by_row = scales_in[w].rearrange("z (q r) n -> r q z n", r=SCALE_ROWS)
             for r in rows:
                 nc.sync.dma_start(
-                    out=w_scales[w][SCALE_ROWS * w + r : P : P // QUADS, :, :].bitcast(I32),
-                    in_=by_row[r].bitcast(I32),
+                    out=w_scales[w][SCALE_ROWS * w + r : P : P // QUADS, passes, :].bitcast(I32),
+                    in_=by_row[r][:, passes, :].bitcast(I32),
                 )
 
-        def load_words(w, passes=slice(0, PASSES)):
-            nc.sync.dma_start(
-                out=w_codes[w][:, passes, :].bitcast(I32),
-                in_=words_in[w][passes].rearrange("z p n t -> p z (n t)").bitcast(I32),
-            )
+        def load_words(w, z):
+            nc.sync.dma_start(out=w_codes[w, z].bitcast(I32), in_=words_in[w][z].rearrange("p n t -> p (n t)").bitcast(I32))
 
         planes = {}
         for i, (z, t0, count) in enumerate(LOADS):
             if i == len(LOADS) - 1:
-                load_scales(2, range(1))
-                load_words(0, slice(0, 1))
+                load_scales(1, range(3, 4), slice(0, 1))
+                load_words(0, 0)
             loaded = keep.tile([P, count * T], F32, name=f"rows{i}", align_bytes=64)
             nc.sync.dma_start(out=loaded[:], in_=x_rows[z, :, t0 : t0 + count, :].rearrange("p t n -> p (t n)"))
             for t in range(count):
                 planes[z, t0 + t] = loaded[:, t * T : (t + 1) * T]
             if i == 0:
                 nc.sync.dma_start(offsets[:], offs)
-            if i in SCALES_BEHIND_LOAD:
-                load_scales(SCALES_BEHIND_LOAD[i])
-        load_words(1, slice(0, 1))
-        load_words(0, slice(1, 2))
-        load_words(1, slice(1, 2))
-        load_scales(2, range(1, SCALE_ROWS))
-        load_words(2)
+                load_scales(0)
+        load_scales(1, range(3))
+        load_words(1, 0)
+        load_words(0, 1)
+        load_words(1, 1)
+        load_scales(1, range(3, 4), slice(1, 2))
+        nc.sync.dma_start(out=third[:].bitcast(I32), in_=w3_words.rearrange("z p n t -> p z (n t)").bitcast(I32))
+        load_scales(2)
 
         pairs = {
             (z, h): keep.tile([P, 2, HALF, 2], BF16, name=f"pairs{z}{h}", align_bytes=64)
@@ -169,7 +169,7 @@ def tile_picked_maxout_max_e_kernel(
             out_rows = slice(m * P, (m + 1) * P)
             nc.tensor.matmul_mx(
                 out=acc,
-                lhsT=w_codes[w][:, z, out_rows].bitcast(FP8X4),
+                lhsT=w_codes[w, z][:, PACK * m * P : PACK * (m + 1) * P].bitcast(FP8X4),
                 lhsT_scale=w_scales[w][SCALE_ROWS * w : P, z, out_rows],
                 rhs=x_codes[z][:, entries].bitcast(FP8X4),
                 rhs_scale=x_scales[z][:, entries],

@@ -28,7 +28,8 @@ SCALE_ROWS = 4
 LIST_ROWS = 16
 PIECES = 4
 PIECE = S // PIECES
-WARM_UPS = [slice(0, S)]
+WARM_UPS = 4
+WARM_ROWS = 32
 
 LOADS = [(0, 0, 4), (1, 0, 2), (1, 2, 1), (1, 3, 1)]
 
@@ -71,16 +72,18 @@ def tile_picked_maxout_max_e_kernel(
         planes = {}
         for i, (z, t0, count) in enumerate(LOADS):
             if i == len(LOADS) - 1:
+                load_scales(1, range(2, 3))
                 load_scales(1, range(3, 4), slice(0, 1))
-                load_words(0, 0)
+                load_scales(0, range(3, 4))
             loaded = keep.tile([P, count * T], F32, name=f"rows{i}", align_bytes=64)
             nc.sync.dma_start(out=loaded[:], in_=x_rows[z, :, t0 : t0 + count, :].rearrange("p t n -> p (t n)"))
             for t in range(count):
                 planes[z, t0 + t] = loaded[:, t * T : (t + 1) * T]
             if i == 0:
                 nc.sync.dma_start(offsets[:], offs)
-                load_scales(0)
-        load_scales(1, range(3))
+                load_scales(0, range(3))
+        load_words(0, 0)
+        load_scales(1, range(2))
         load_words(1, 0)
         load_words(0, 1)
         load_words(1, 1)
@@ -228,10 +231,18 @@ def tile_picked_maxout_max_e_kernel(
             for c in range(1, PIECES):
                 piece_pass(w, c, 0)
 
-        opening_passes(0)
         warm = psum.tile([P, S], F32, name="warm", tag="bank7")
-        for entries in WARM_UPS:
-            one_pass(warm[:, entries], 0, 0, 0, entries, start=True, stop=True)
+        for i in range(WARM_UPS):
+            nc.tensor.matmul_mx(
+                out=warm[0:WARM_ROWS, :],
+                lhsT=x_codes[0][:, 0:WARM_ROWS].bitcast(FP8X4),
+                lhsT_scale=w_scales[0][:, 0, 0:WARM_ROWS],
+                rhs=x_codes[0][:].bitcast(FP8X4),
+                rhs_scale=x_scales[0][:],
+                start=True,
+                stop=True,
+            )
+        opening_passes(0)
         opening_passes(1)
         reduce_first_piece(0)
         w1_out(1)

@@ -28,6 +28,7 @@ SCALE_ROWS = 4
 LIST_ROWS = 16
 PIECES = 4
 PIECE = S // PIECES
+ON_VECTOR = 256
 WARM_UPS = 4
 WARM_ROWS = 32
 
@@ -72,9 +73,9 @@ def tile_picked_maxout_max_e_kernel(
         planes = {}
         for i, (z, t0, count) in enumerate(LOADS):
             if i == len(LOADS) - 1:
+                load_scales(0, range(3, 4))
                 load_scales(1, range(2, 3))
                 load_scales(1, range(3, 4), slice(0, 1))
-                load_scales(0, range(3, 4))
             loaded = keep.tile([P, count * T], F32, name=f"rows{i}", align_bytes=64)
             nc.sync.dma_start(out=loaded[:], in_=x_rows[z, :, t0 : t0 + count, :].rearrange("p t n -> p (t n)"))
             for t in range(count):
@@ -91,79 +92,62 @@ def tile_picked_maxout_max_e_kernel(
         nc.sync.dma_start(out=third[:].bitcast(I32), in_=w3_words.rearrange("z p n t -> p z (n t)").bitcast(I32))
         load_scales(2)
 
-        pairs = {
-            (z, h): keep.tile([P, 2, HALF, 2], BF16, name=f"pairs{z}{h}", align_bytes=64)
-            for z in range(PASSES)
-            for h in range(HALVES)
-        }
-        x_codes, x_scales, woven = {}, {}, {}
-        for z in range(PASSES):
-            x_codes[z] = keep.tile([P, S], U32, name=f"codes{z}", align_bytes=64)
-            x_scales[z] = keep.tile([P, S], U8, name=f"scales{z}", align_bytes=64)
-            for h in range(HALVES):
-                if z == 0:
-                    woven[z, h] = pairs[1, h][:].rearrange("p u n e -> p (u n e)")
-                else:
-                    woven[z, h] = keep.tile([P, PACK * HALF], BF16, name=f"woven{z}{h}", align_bytes=64)[:]
+        x_codes = [keep.tile([P, S], U32, name=f"codes{z}", align_bytes=64) for z in range(PASSES)]
+        x_scales = [keep.tile([P, S], U8, name=f"scales{z}", align_bytes=64) for z in range(PASSES)]
+        front = keep.tile([P, S - PIECE, PACK], BF16, name="front", align_bytes=64)
+        back = keep.tile([P, PIECE, PACK], BF16, name="back", align_bytes=64)
+        on_scalar = [slice(ON_VECTOR, S - PIECE), slice(S - PIECE, S)]
 
-        def gather(z, t, h):
-            nc.vector.tensor_copy(
-                out=pairs[z, h][:, t // 2, :, t % 2],
-                in_=planes[z, t].indirect(offsets[:, h * HALF // LIST_ROWS : (h + 1) * HALF // LIST_ROWS]),
+        def places(entries):
+            if entries.start < S - PIECE:
+                return front[:, entries, :]
+            return back[:, entries.start - (S - PIECE) : entries.stop - (S - PIECE), :]
+
+        def listed(z, t, entries):
+            return planes[z, t].indirect(offsets[:, entries.start // LIST_ROWS : entries.stop // LIST_ROWS])
+
+        def gather_on_vector(z, t):
+            nc.vector.tensor_copy(out=front[:, 0:ON_VECTOR, t], in_=listed(z, t, slice(0, ON_VECTOR)))
+
+        def gather_on_scalar(picked, z, t, entries):
+            nc.scalar.activation(
+                out=picked[:, entries.start - ON_VECTOR : entries.stop - ON_VECTOR], in_=listed(z, t, entries), func=COPY
             )
 
-        def weave(z, h, piece):
-            pair_words = pairs[z, h][:].rearrange("p u n e -> p (u n e)").bitcast(U32).rearrange("p (u n) -> p n u", u=2)
-            for j in range(0, HALF, piece):
-                nc.scalar.copy(
-                    out=woven[z, h][:, PACK * j : PACK * (j + piece)].bitcast(U32).rearrange("p (n u) -> p n u", u=2),
-                    in_=pair_words[:, j : j + piece, :],
-                )
+        def place_on_scalar(picked, t0, entries):
+            count = picked.shape[1]
+            nc.scalar.copy(
+                out=places(entries)[:, :, t0 : t0 + count],
+                in_=picked[:, :, entries.start - ON_VECTOR : entries.stop - ON_VECTOR].rearrange("p t n -> p n t"),
+            )
 
-        def quantise(z, h, piece):
-            for j in range(0, HALF, piece):
-                entries = slice(h * HALF + j, h * HALF + j + piece)
-                nc.vector.quantize_mx(
-                    out=x_codes[z][:, entries].bitcast(FP8X4),
-                    scales=x_scales[z][:, entries],
-                    in_=woven[z, h][:, PACK * j : PACK * (j + piece)],
-                )
+        def quantise(z, entries):
+            nc.vector.quantize_mx(
+                out=x_codes[z][:, entries].bitcast(FP8X4),
+                scales=x_scales[z][:, entries],
+                in_=places(entries).rearrange("p n t -> p (n t)"),
+            )
 
-        def gather_on_scalar(z, u):
-            picked = keep.tile([P, 2, HALF], F32, name=f"picked{z}", align_bytes=64)
-            for e in range(2):
-                nc.scalar.activation(
-                    out=picked[:, e, :], in_=planes[z, 2 * u + e].indirect(offsets[:, HALF // LIST_ROWS :]), func=COPY
-                )
-            nc.scalar.copy(out=pairs[z, 1][:, u, :, :], in_=picked[:].rearrange("p e n -> p n e"))
-
-        gather_on_scalar(0, 1)
-        for t, h in [(0, 1), (0, 0), (1, 1), (1, 0), (2, 0), (3, 0)]:
-            gather(0, t, h)
-        for h in reversed(range(HALVES)):
-            weave(0, h, HALF)
-        for h in reversed(range(HALVES)):
-            quantise(0, h, HALF)
-        gather_on_scalar(1, 0)
-        for t, h in [(0, 0), (1, 0), (2, 0), (2, 1)]:
-            gather(1, t, h)
-        for h in range(HALVES):
-            weave(1, h, HALF)
-
-        def last_slot(h):
-            return woven[1, h].rearrange("p (n t) -> p n t", t=PACK)[:, :, PACK - 1]
-
-        def listed(first_entry, entries):
-            return planes[1, 3].indirect(offsets[:, first_entry // LIST_ROWS : (first_entry + entries) // LIST_ROWS])
-
-        nc.vector.tensor_copy(out=last_slot(0), in_=listed(0, HALF))
-        dense = [keep.tile([P, PIECE], BF16, name=f"dense{j}", align_bytes=64)[:] for j in range(2)]
-        for j in range(2):
-            nc.scalar.activation(out=dense[j], in_=listed(HALF + j * PIECE, PIECE), func=COPY)
-        for j in range(2):
-            nc.scalar.copy(out=last_slot(1)[:, j * PIECE : (j + 1) * PIECE], in_=dense[j])
-        for h in range(HALVES):
-            quantise(1, h, HALF // 2)
+        for z, count in [(0, PACK), (1, 2)]:
+            picked = keep.tile([P, count, S - ON_VECTOR], F32, name=f"picked{z}", align_bytes=64)
+            for t in range(count):
+                gather_on_vector(z, t)
+                gather_on_scalar(picked[:, t, :], z, t, slice(ON_VECTOR, S))
+            for entries in on_scalar:
+                place_on_scalar(picked[:], 0, entries)
+            if z == 0:
+                quantise(0, slice(0, S - PIECE))
+                quantise(0, slice(S - PIECE, S))
+        picked = keep.tile([P, 2, S - ON_VECTOR], BF16, name="picked_last", align_bytes=64)
+        gather_on_vector(1, 2)
+        gather_on_scalar(picked[:, 0, :], 1, 2, slice(ON_VECTOR, S))
+        gather_on_vector(1, 3)
+        for entries in on_scalar:
+            gather_on_scalar(picked[:, 1, :], 1, 3, entries)
+        for entries in on_scalar:
+            place_on_scalar(picked[:], 2, entries)
+        for c in range(PIECES):
+            quantise(1, slice(c * PIECE, (c + 1) * PIECE))
 
 
         tiles = range(M_TILES)

@@ -73,16 +73,17 @@ def tile_picked_maxout_max_e_kernel(
         planes = {}
         for i, (z, t0, count) in enumerate(LOADS):
             if i == len(LOADS) - 1:
-                load_scales(0, range(3, 4))
-                load_scales(1, range(2, 3))
-                load_scales(1, range(3, 4), slice(0, 1))
+                for w, r, scale_pass in [(0, 3, 0), (0, 2, 1), (0, 3, 1), (1, 2, 0), (1, 2, 1), (1, 3, 0)]:
+                    load_scales(w, range(r, r + 1), slice(scale_pass, scale_pass + 1))
             loaded = keep.tile([P, count * T], F32, name=f"rows{i}", align_bytes=64)
             nc.sync.dma_start(out=loaded[:], in_=x_rows[z, :, t0 : t0 + count, :].rearrange("p t n -> p (t n)"))
             for t in range(count):
                 planes[z, t0 + t] = loaded[:, t * T : (t + 1) * T]
             if i == 0:
                 nc.sync.dma_start(offsets[:], offs)
-                load_scales(0, range(3))
+                load_scales(0, range(3), slice(0, 1))
+            if i == 1:
+                load_scales(0, range(2), slice(1, 2))
         load_words(0, 0)
         load_scales(1, range(2))
         load_words(1, 0)

@@ -172,12 +172,13 @@ def tile_picked_maxout_max_e_kernel(
             one_pass(both[m][:, w, :], w, m, z, slice(0, PIECE), start=(w, z) == (0, 0), stop=(w, z) == (1, 1))
 
         def piece_pass(w, c, z):
-            if z == 0:
+            opens = (w, c) not in acc
+            if opens:
                 acc[w, c] = psum.tile([P, M_TILES, PIECE], F32, name=f"acc{w}{c}", tag=f"bank{PIECES * w + c}")
             for m in tiles:
                 one_pass(
                     acc[w, c][:, m, :], w, m, z, slice(c * PIECE, (c + 1) * PIECE),
-                    start=(z == 0 and m == 0), stop=(z == PASSES - 1 and m == M_TILES - 1),
+                    start=(opens and m == 0), stop=(not opens and m == M_TILES - 1),
                 )
 
         of_w12 = [keep.tile([P, M_TILES, HALF], F32, name=f"two{h}") for h in range(HALVES)]
@@ -198,6 +199,8 @@ def tile_picked_maxout_max_e_kernel(
 
         def first_max(c):
             piece_pass(1, c, 1)
+            if c == PIECES - 1:
+                piece_pass(1, c, 0)
             h, j = divmod(c * PIECE, HALF)
             nc.vector.tensor_tensor(of_w12[h][:, :, j : j + PIECE], acc[1, c][:], of_w1[c][:], MAX)
 
@@ -213,7 +216,7 @@ def tile_picked_maxout_max_e_kernel(
         def opening_passes(w):
             for m in tiles:
                 first_piece_pass(w, m, 0)
-            for c in range(1, PIECES):
+            for c in range(1, PIECES - w):
                 piece_pass(w, c, 0)
 
         warm = psum.tile([P, S], F32, name="warm", tag="bank7")

@@ -129,24 +129,29 @@ def tile_picked_maxout_max_e_kernel(
                 in_=places(entries).rearrange("p n t -> p (n t)"),
             )
 
-        for z, count in [(0, PACK), (1, 2)]:
-            picked = keep.tile([P, count, S - ON_VECTOR], F32, name=f"picked{z}", align_bytes=64)
-            for t in range(count):
-                gather_on_vector(z, t)
-                gather_on_scalar(picked[:, t, :], z, t, slice(ON_VECTOR, S))
-            for entries in on_scalar:
-                place_on_scalar(picked[:], 0, entries)
-            if z == 0:
-                quantise(0, slice(0, S - PIECE))
-                quantise(0, slice(S - PIECE, S))
+        picked = keep.tile([P, PACK, S - ON_VECTOR], F32, name="picked0", align_bytes=64)
+        for t in range(PACK):
+            gather_on_vector(0, t)
+            gather_on_scalar(picked[:, t, :], 0, t, slice(ON_VECTOR, S))
+        for entries in on_scalar:
+            place_on_scalar(picked[:], 0, entries)
+        quantise(0, slice(0, S - PIECE))
+        quantise(0, slice(S - PIECE, S))
+        picked = keep.tile([P, 2, S - ON_VECTOR], F32, name="picked1", align_bytes=64)
+        for t in range(2):
+            nc.vector.tensor_copy(out=front[:, :, t], in_=listed(1, t, slice(0, S - PIECE)))
+            gather_on_scalar(picked[:, t, :], 1, t, on_scalar[1])
+        place_on_scalar(picked[:], 0, on_scalar[1])
         picked = keep.tile([P, 2, S - ON_VECTOR], BF16, name="picked_last", align_bytes=64)
         gather_on_vector(1, 2)
         gather_on_scalar(picked[:, 0, :], 1, 2, slice(ON_VECTOR, S))
+        for entries in on_scalar:
+            place_on_scalar(picked[:, 0:1, :], 2, entries)
         gather_on_vector(1, 3)
         for entries in on_scalar:
             gather_on_scalar(picked[:, 1, :], 1, 3, entries)
         for entries in on_scalar:
-            place_on_scalar(picked[:], 2, entries)
+            place_on_scalar(picked[:, 1:2, :], 3, entries)
         for c in range(PIECES):
             quantise(1, slice(c * PIECE, (c + 1) * PIECE))
 

@@ -48,13 +48,13 @@ def tile_picked_maxout_max_e_kernel(
         psum = ctx.enter_context(tc.psum_pool(name="psum", bufs=1))
 
         offsets = keep.tile([P, S // LIST_ROWS], U16, name="offsets")
-        packed = keep.tile([P, 5, N], U8, name="packed", align_bytes=64)
+        packed = keep.tile([P, 5, N], U8, name="packed", align_bytes=256)
         nc.vector.memset(packed[:, 0:3, :].bitcast(I32), 0)
         nc.scalar.copy(out=packed[:, 3:5, :].bitcast(U32), in_=packed[:, 0:2, :].bitcast(U32))
         w_scales = [packed[:, 0:3:2, :], packed[:, 1:3, :], packed[:, 3:5, :]]
-        late = keep.tile([P, 2, PACK * N], U8, name="late", align_bytes=64)
-        first = [keep.tile([P, PACK * N], U8, name=f"first_words{w}", align_bytes=64) for w in range(2)]
-        third = keep.tile([P, PASSES, PACK * N], U8, name="third", align_bytes=64)
+        late = keep.tile([P, 2, PACK * N], U8, name="late", align_bytes=256)
+        first = [keep.tile([P, PACK * N], U8, name=f"first_words{w}", align_bytes=256) for w in range(2)]
+        third = keep.tile([P, PASSES, PACK * N], U8, name="third", align_bytes=256)
         w_codes = {(w, 0): first[w][:] for w in range(2)}
         w_codes.update({(w, 1): late[:, w, :] for w in range(2)})
         w_codes.update({(2, z): third[:, z, :] for z in range(PASSES)})
@@ -75,7 +75,7 @@ def tile_picked_maxout_max_e_kernel(
             if i == len(LOADS) - 1:
                 for w, r, scale_pass in [(0, 3, 0), (0, 2, 1), (0, 3, 1), (1, 2, 0), (1, 2, 1), (1, 3, 0)]:
                     load_scales(w, range(r, r + 1), slice(scale_pass, scale_pass + 1))
-            loaded = keep.tile([P, count * T], F32, name=f"rows{i}", align_bytes=64)
+            loaded = keep.tile([P, count * T], F32, name=f"rows{i}", align_bytes=256)
             nc.sync.dma_start(out=loaded[:], in_=x_rows[z, :, t0 : t0 + count, :].rearrange("p t n -> p (t n)"))
             for t in range(count):
                 planes[z, t0 + t] = loaded[:, t * T : (t + 1) * T]
@@ -93,10 +93,10 @@ def tile_picked_maxout_max_e_kernel(
         nc.sync.dma_start(out=third[:].bitcast(I32), in_=w3_words.rearrange("z p n t -> p z (n t)").bitcast(I32))
         load_scales(2)
 
-        x_codes = [keep.tile([P, S], U32, name=f"codes{z}", align_bytes=64) for z in range(PASSES)]
-        x_scales = [keep.tile([P, S], U8, name=f"scales{z}", align_bytes=64) for z in range(PASSES)]
-        front = keep.tile([P, S - PIECE, PACK], BF16, name="front", align_bytes=64)
-        back = keep.tile([P, PIECE, PACK], BF16, name="back", align_bytes=64)
+        x_codes = [keep.tile([P, S], U32, name=f"codes{z}", align_bytes=256) for z in range(PASSES)]
+        x_scales = [keep.tile([P, S], U8, name=f"scales{z}", align_bytes=256) for z in range(PASSES)]
+        front = keep.tile([P, S - PIECE, PACK], BF16, name="front", align_bytes=256)
+        back = keep.tile([P, PIECE, PACK], BF16, name="back", align_bytes=256)
         on_scalar = [slice(ON_VECTOR, S - PIECE), slice(S - PIECE, S)]
 
         def places(entries):
@@ -129,7 +129,7 @@ def tile_picked_maxout_max_e_kernel(
                 in_=places(entries).rearrange("p n t -> p (n t)"),
             )
 
-        picked = keep.tile([P, PACK, S - ON_VECTOR], F32, name="picked0", align_bytes=64)
+        picked = keep.tile([P, PACK, S - ON_VECTOR], F32, name="picked0", align_bytes=256)
         for t in range(PACK):
             gather_on_vector(0, t)
             gather_on_scalar(picked[:, t, :], 0, t, slice(ON_VECTOR, S))
@@ -137,12 +137,12 @@ def tile_picked_maxout_max_e_kernel(
             place_on_scalar(picked[:], 0, entries)
         quantise(0, slice(0, S - PIECE))
         quantise(0, slice(S - PIECE, S))
-        picked = keep.tile([P, 2, S - ON_VECTOR], F32, name="picked1", align_bytes=64)
+        picked = keep.tile([P, 2, S - ON_VECTOR], F32, name="picked1", align_bytes=256)
         for t in range(2):
             nc.vector.tensor_copy(out=front[:, :, t], in_=listed(1, t, slice(0, S - PIECE)))
             gather_on_scalar(picked[:, t, :], 1, t, on_scalar[1])
         place_on_scalar(picked[:], 0, on_scalar[1])
-        picked = keep.tile([P, 2, S - ON_VECTOR], BF16, name="picked_last", align_bytes=64)
+        picked = keep.tile([P, 2, S - ON_VECTOR], BF16, name="picked_last", align_bytes=256)
         gather_on_vector(1, 2)
         gather_on_scalar(picked[:, 0, :], 1, 2, slice(ON_VECTOR, S))
         for entries in on_scalar:
@@ -214,7 +214,7 @@ def tile_picked_maxout_max_e_kernel(
             of_w3 = psum.tile([P, HALF], F32, name=f"third{h}{m}", tag=f"bank{bank}")
             for z in range(PASSES):
                 one_pass(of_w3[:], 2, m, z, entries, start=(z == 0), stop=(z == PASSES - 1))
-            result = keep.tile([P, HALF], F32, name=f"three{h}{m}")
+            result = keep.tile([P, HALF], F32, name=f"three{h}{m}", align_bytes=256)
             nc.vector.tensor_tensor(result[:], of_w3[:], of_w12[h][:, m, :], MAX)
             nc.sync.dma_start(out=out[m * P : (m + 1) * P, entries], in_=result[:])
 

@@ -93,8 +93,10 @@ def tile_picked_maxout_max_e_kernel(
         nc.sync.dma_start(out=third[:].bitcast(I32), in_=w3_words.rearrange("z p n t -> p z (n t)").bitcast(I32))
         load_scales(2)
 
-        x_codes = [keep.tile([P, S], U32, name=f"codes{z}", align_bytes=256) for z in range(PASSES)]
-        x_scales = [keep.tile([P, S], U8, name=f"scales{z}", align_bytes=256) for z in range(PASSES)]
+        code_tiles = [keep.tile([P, S + 32], U32, name=f"codes{z}", align_bytes=256) for z in range(PASSES)]
+        scale_tiles = [keep.tile([P, S + 64], U8, name=f"scales{z}", align_bytes=256) for z in range(PASSES)]
+        x_codes = [tile[:, 32:] for tile in code_tiles]
+        x_scales = [tile[:, 64:] for tile in scale_tiles]
         front = keep.tile([P, S - PIECE, PACK], BF16, name="front", align_bytes=256)
         back = keep.tile([P, PIECE, PACK], BF16, name="back", align_bytes=256)
         on_scalar = [slice(ON_VECTOR, S - PIECE), slice(S - PIECE, S)]

from contextlib import ExitStack

import concourse.mybir as mybir

K, T, S, N = 1024, 2048, 512, 256
FLOPS = 3 * 2 * K * S * N

F32 = mybir.dt.float32
BF16 = mybir.dt.bfloat16
I32 = mybir.dt.int32
U32 = mybir.dt.uint32
U16 = mybir.dt.uint16
U8 = mybir.dt.uint8
FP8X4 = mybir.dt.float8_e4m3fn_x4
COPY = mybir.ActivationFunctionType.Copy
MAX = mybir.AluOpType.max
AXIS_X = mybir.AxisListType.X

P = 128
PACK = 4
PASSES = K // (P * PACK)
WEIGHTS = 3
HALVES = 2
HALF = S // HALVES
M_TILES = N // P
QUADS = 4
SCALE_ROWS = 4
LIST_ROWS = 16
PIECES = 4
PIECE = S // PIECES
ON_VECTOR = 256
WARM_UPS = 4
WARM_ROWS = 32

LOADS = [(0, 0, 4), (1, 0, 2), (1, 2, 1), (1, 3, 1)]


def tile_picked_maxout_max_e_kernel(
    tc, xT, w1_words, w1_scales, w2_words, w2_scales, w3_words, w3_scales, offs, out
):
    nc = tc.nc
    words_in = (w1_words, w2_words, w3_words)
    scales_in = (w1_scales, w2_scales, w3_scales)
    x_rows = xT.rearrange("(z p t) n -> z p t n", z=PASSES, t=PACK)

    with ExitStack() as ctx:
        keep = ctx.enter_context(tc.tile_pool(name="keep", bufs=1))
        psum = ctx.enter_context(tc.psum_pool(name="psum", bufs=1))

        offsets = keep.tile([P, S // LIST_ROWS], U16, name="offsets")
        packed = keep.tile([P, 5, N], U8, name="packed", align_bytes=256)
        nc.vector.memset(packed[:, 0:3, :].bitcast(I32), 0)
        nc.scalar.copy(out=packed[:, 3:5, :].bitcast(U32), in_=packed[:, 0:2, :].bitcast(U32))
        w_scales = [packed[:, 0:3:2, :], packed[:, 1:3, :], packed[:, 3:5, :]]
        late = keep.tile([P, 2, PACK * N], U8, name="late", align_bytes=256)
        first = [keep.tile([P, PACK * N], U8, name=f"first_words{w}", align_bytes=256) for w in range(2)]
        third = keep.tile([P, PASSES, PACK * N], U8, name="third", align_bytes=256)
        w_codes = {(w, 0): first[w][:] for w in range(2)}
        w_codes.update({(w, 1): late[:, w, :] for w in range(2)})
        w_codes.update({(2, z): third[:, z, :] for z in range(PASSES)})

        def load_scales(w, rows=range(SCALE_ROWS), passes=slice(0, PASSES)):
            by_row = scales_in[w].rearrange("z (q r) n -> r q z n", r=SCALE_ROWS)
            for r in rows:
                nc.sync.dma_start(
                    out=w_scales[w][SCALE_ROWS * w + r : P : P // QUADS, passes, :].bitcast(I32),
                    in_=by_row[r][:, passes, :].bitcast(I32),
                )

        def load_words(w, z):
            nc.sync.dma_start(out=w_codes[w, z].bitcast(I32), in_=words_in[w][z].rearrange("p n t -> p (n t)").bitcast(I32))

        planes = {}
        for i, (z, t0, count) in enumerate(LOADS):
            if i == len(LOADS) - 1:
                for w, r, scale_pass in [(0, 3, 0), (0, 2, 1), (0, 3, 1), (1, 2, 0), (1, 2, 1), (1, 3, 0)]:
                    load_scales(w, range(r, r + 1), slice(scale_pass, scale_pass + 1))
            loaded = keep.tile([P, count * T], F32, name=f"rows{i}", align_bytes=256)
            nc.sync.dma_start(out=loaded[:], in_=x_rows[z, :, t0 : t0 + count, :].rearrange("p t n -> p (t n)"))
            for t in range(count):
                planes[z, t0 + t] = loaded[:, t * T : (t + 1) * T]
            if i == 0:
                nc.sync.dma_start(offsets[:], offs)
                load_scales(0, range(3), slice(0, 1))
            if i == 1:
                load_scales(0, range(2), slice(1, 2))
        load_words(0, 0)
        load_scales(1, range(2))
        load_words(1, 0)
        load_words(0, 1)
        load_words(1, 1)
        load_scales(1, range(3, 4), slice(1, 2))
        nc.sync.dma_start(out=third[:].bitcast(I32), in_=w3_words.rearrange("z p n t -> p z (n t)").bitcast(I32))
        load_scales(2)

        code_tiles = [keep.tile([P, S + 32], U32, name=f"codes{z}", align_bytes=256) for z in range(PASSES)]
        scale_tiles = [keep.tile([P, S + 64], U8, name=f"scales{z}", align_bytes=256) for z in range(PASSES)]
        x_codes = [tile[:, 32:] for tile in code_tiles]
        x_scales = [tile[:, 64:] for tile in scale_tiles]
        front = keep.tile([P, S - PIECE, PACK], BF16, name="front", align_bytes=256)
        back = keep.tile([P, PIECE, PACK], BF16, name="back", align_bytes=256)
        on_scalar = [slice(ON_VECTOR, S - PIECE), slice(S - PIECE, S)]

        def places(entries):
            if entries.start < S - PIECE:
                return front[:, entries, :]
            return back[:, entries.start - (S - PIECE) : entries.stop - (S - PIECE), :]

        def listed(z, t, entries):
            return planes[z, t].indirect(offsets[:, entries.start // LIST_ROWS : entries.stop // LIST_ROWS])

        def gather_on_vector(z, t):
            nc.vector.tensor_copy(out=front[:, 0:ON_VECTOR, t], in_=listed(z, t, slice(0, ON_VECTOR)))

        def gather_on_scalar(picked, z, t, entries):
            nc.scalar.activation(
                out=picked[:, entries.start - ON_VECTOR : entries.stop - ON_VECTOR], in_=listed(z, t, entries), func=COPY
            )

        def place_on_scalar(picked, t0, entries):
            count = picked.shape[1]
            nc.scalar.copy(
                out=places(entries)[:, :, t0 : t0 + count],
                in_=picked[:, :, entries.start - ON_VECTOR : entries.stop - ON_VECTOR].rearrange("p t n -> p n t"),
            )

        def quantise(z, entries):
            nc.vector.quantize_mx(
                out=x_codes[z][:, entries].bitcast(FP8X4),
                scales=x_scales[z][:, entries],
                in_=places(entries).rearrange("p n t -> p (n t)"),
            )

        picked = keep.tile([P, PACK, S - ON_VECTOR], F32, name="picked0", align_bytes=256)
        for t in range(PACK):
            gather_on_vector(0, t)
            gather_on_scalar(picked[:, t, :], 0, t, slice(ON_VECTOR, S))
        for entries in on_scalar:
            place_on_scalar(picked[:], 0, entries)
        quantise(0, slice(0, S - PIECE))
        quantise(0, slice(S - PIECE, S))
        picked = keep.tile([P, 2, S - ON_VECTOR], F32, name="picked1", align_bytes=256)
        for t in range(2):
            nc.vector.tensor_copy(out=front[:, :, t], in_=listed(1, t, slice(0, S - PIECE)))
            gather_on_scalar(picked[:, t, :], 1, t, on_scalar[1])
        place_on_scalar(picked[:], 0, on_scalar[1])
        picked = keep.tile([P, 2, S - ON_VECTOR], BF16, name="picked_last", align_bytes=256)
        gather_on_vector(1, 2)
        gather_on_scalar(picked[:, 0, :], 1, 2, slice(ON_VECTOR, S))
        for entries in on_scalar:
            place_on_scalar(picked[:, 0:1, :], 2, entries)
        gather_on_vector(1, 3)
        for entries in on_scalar:
            gather_on_scalar(picked[:, 1, :], 1, 3, entries)
        for entries in on_scalar:
            place_on_scalar(picked[:, 1:2, :], 3, entries)
        for c in range(PIECES):
            quantise(1, slice(c * PIECE, (c + 1) * PIECE))


        tiles = range(M_TILES)

        def one_pass(acc, w, m, z, entries, start, stop):
            out_rows = slice(m * P, (m + 1) * P)
            nc.tensor.matmul_mx(
                out=acc,
                lhsT=w_codes[w, z][:, PACK * m * P : PACK * (m + 1) * P].bitcast(FP8X4),
                lhsT_scale=w_scales[w][SCALE_ROWS * w : P, z, out_rows],
                rhs=x_codes[z][:, entries].bitcast(FP8X4),
                rhs_scale=x_scales[z][:, entries],
                start=start,
                stop=stop,
            )

        both = [psum.tile([P, 2, PIECE], F32, name=f"both{m}", tag=f"bank{PIECES * m}") for m in tiles]
        acc = {}

        def first_piece_pass(w, m, z):
            one_pass(both[m][:, w, :], w, m, z, slice(0, PIECE), start=(w, z) == (0, 0), stop=(w, z) == (1, 1))

        def piece_pass(w, c, z):
            opens = (w, c) not in acc
            if opens:
                acc[w, c] = psum.tile([P, M_TILES, PIECE], F32, name=f"acc{w}{c}", tag=f"bank{PIECES * w + c}")
            for m in tiles:
                one_pass(
                    acc[w, c][:, m, :], w, m, z, slice(c * PIECE, (c + 1) * PIECE),
                    start=(opens and m == 0), stop=(not opens and m == M_TILES - 1),
                )

        of_w12 = [keep.tile([P, M_TILES, HALF], F32, name=f"two{h}") for h in range(HALVES)]

        def reduce_first_piece(m):
            for w in range(2):
                first_piece_pass(w, m, 1)
            nc.vector.tensor_reduce(
                out=of_w12[0][:, m, 0:PIECE], in_=both[m][:].rearrange("p w n -> p n w"), axis=AXIS_X, op=MAX
            )

        of_w1 = {}

        def w1_out(c):
            piece_pass(0, c, 1)
            of_w1[c] = keep.tile([P, M_TILES, PIECE], F32, name=f"first{c}")
            nc.scalar.copy(out=of_w1[c][:], in_=acc[0, c][:])

        def first_max(c):
            piece_pass(1, c, 1)
            if c == PIECES - 1:
                piece_pass(1, c, 0)
            h, j = divmod(c * PIECE, HALF)
            nc.vector.tensor_tensor(of_w12[h][:, :, j : j + PIECE], acc[1, c][:], of_w1[c][:], MAX)

        def finish(h, m, bank):
            entries = slice(h * HALF, (h + 1) * HALF)
            of_w3 = psum.tile([P, HALF], F32, name=f"third{h}{m}", tag=f"bank{bank}")
            for z in range(PASSES):
                one_pass(of_w3[:], 2, m, z, entries, start=(z == 0), stop=(z == PASSES - 1))
            result = keep.tile([P, HALF], F32, name=f"three{h}{m}", align_bytes=256)
            nc.vector.tensor_tensor(result[:], of_w3[:], of_w12[h][:, m, :], MAX)
            nc.sync.dma_start(out=out[m * P : (m + 1) * P, entries], in_=result[:])

        def opening_passes(w):
            for m in tiles:
                first_piece_pass(w, m, 0)
            for c in range(1, PIECES - w):
                piece_pass(w, c, 0)

        warm = psum.tile([P, S], F32, name="warm", tag="bank7")
        for i in range(WARM_UPS):
            nc.tensor.matmul_mx(
                out=warm[0:WARM_ROWS, :],
                lhsT=x_codes[0][:, 0:WARM_ROWS].bitcast(FP8X4),
                lhsT_scale=w_scales[0][:, 0, 0:WARM_ROWS],
                rhs=x_codes[0][:].bitcast(FP8X4),
                rhs_scale=x_scales[0][:],
                start=True,
                stop=True,
            )
        opening_passes(0)
        opening_passes(1)
        reduce_first_piece(0)
        w1_out(1)
        reduce_first_piece(1)
        for c in range(1, PIECES):
            if c + 1 < PIECES:
                w1_out(c + 1)
            first_max(c)
        finish(0, 0, 0)
        finish(0, 1, PIECES)
        finish(1, 0, 1)
        finish(1, 1, 2)
